import numpy as np
import ml_dtypes


def mxq(x, axis, fmt="e4m3"):
    dtype, down = {"e4m3": (ml_dtypes.float8_e4m3fn, 7), "e5m2": (ml_dtypes.float8_e5m2, 14)}[fmt]
    v = np.moveaxis(np.asarray(x, np.float32).astype(ml_dtypes.bfloat16).astype(np.float64), axis, -1)
    blocks = v.reshape(v.shape[:-1] + (-1, 32))
    amax = np.abs(blocks).max(-1, keepdims=True)
    byte = np.maximum(np.where(amax > 0, np.frexp(amax)[1] - 1 + 127, 0) - down, 1)
    scale = np.exp2(byte - 127.0)
    codes = (blocks / scale).astype(np.float32).astype(dtype).astype(np.float64)
    return np.moveaxis((codes * scale).reshape(v.shape), -1, axis)


WIDE = False


def mx_kscale(k):
    if not WIDE:
        return np.ones(k)
    levels = np.array([10, -10, 5, -5, 0])
    if k % 512:
        return np.exp2(np.random.permutation(np.resize(levels, k // 32))).repeat(32)
    a = np.empty((k // 512, 16))
    for p in range(k // 512):
        a[p, :8] = np.random.permutation(np.resize(levels, 8))
        for g in range(8):
            far = levels[np.abs(levels - a[p, g]) >= 10]
            a[p, g + 8] = far[np.random.randint(len(far))]
    return np.exp2(a.ravel()).repeat(32)


BF16 = ml_dtypes.bfloat16


def bf(x):
    return np.asarray(x, np.float32).astype(BF16)


def f64(x):
    return np.asarray(x).astype(np.float64)


E2M1 = np.array([0.0, 0.5, 1.0, 1.5, 2.0, 3.0, 4.0, 6.0, -0.0, -0.5, -1.0, -1.5, -2.0, -3.0, -4.0, -6.0])


def pack_weight(w, fmt):
    k, n = w.shape
    w = f64(bf(w)).reshape(k // 32, 32, n)
    amax = np.abs(w).max(1)
    if fmt == "e4m3":
        byte = np.frexp(amax)[1] - 1 + 127 - 7
    else:
        mant, ex = np.frexp(amax / 6.0)
        byte = np.where(mant > 0.5, ex, ex - 1) + 127
    byte = np.clip(np.where(amax > 0, byte, 1), 1, 254)
    scaled = (w * np.exp2(127.0 - byte)[:, None, :]).reshape(k, n).astype(np.float32)
    by_word = np.ascontiguousarray(scaled.reshape(k // 512, 128, 4, n).transpose(0, 1, 3, 2))
    if fmt == "e4m3":
        words = by_word.astype(ml_dtypes.float8_e4m3fn).view(np.uint8)
    else:
        c = by_word.astype(ml_dtypes.float4_e2m1fn).view(np.uint8) & 0xF
        words = c[..., 0::2] | (c[..., 1::2] << 4)
    return np.ascontiguousarray(words), np.ascontiguousarray(byte.astype(np.uint8).reshape(k // 512, 16, n))


def unpack_weight(words, scales, fmt):
    g, p, n, _ = words.shape
    if fmt == "e4m3":
        vals = np.ascontiguousarray(words).view(ml_dtypes.float8_e4m3fn).astype(np.float64)
    else:
        nib = np.empty((g, p, n, 4), np.uint8)
        nib[..., 0::2] = words & 0xF
        nib[..., 1::2] = words >> 4
        vals = E2M1[nib]
    vals = vals * np.repeat(np.exp2(scales.astype(np.float64) - 127.0), 8, axis=1)[..., None]
    return vals.transpose(0, 1, 3, 2).reshape(g * 512, n)
def pack4(w):
    words, scales = pack_weight(w, "e2m1")
    return words.reshape(words.shape[0], 128, -1), scales


def unpack4(words, scales):
    return unpack_weight(words.reshape(words.shape[0], 128, -1, 2), scales, "e2m1")


def planes(Y):
    n, m = Y.shape
    b = f64(bf(Y)).reshape(n // 32, 32, m)
    amax = np.abs(b).max(1)
    byte = np.clip(np.where(amax > 0, np.frexp(amax)[1] - 1 + 127 - 7, 1), 1, 254)
    codes = (b * np.exp2(127.0 - byte)[:, None, :]).reshape(n, m).astype(np.float32).astype(ml_dtypes.float8_e4m3fn).view(np.uint8)
    words = codes.reshape(n // 512, 128, 4, m).transpose(0, 1, 3, 2)
    return np.ascontiguousarray(words), np.ascontiguousarray(byte.astype(np.uint8).reshape(n // 512, 16, m))


T, D, F, L = 2048, 1024, 1536, 256


def setup_inputs():
    s = mx_kscale(D)
    t = mx_kscale(T)
    x = np.random.randn(D, T) * s[:, None]
    w = np.random.randn(D, F) / np.sqrt(D) / s[:, None]
    omega = np.random.randn(D, L) / np.sqrt(D) / s[:, None]
    x_words, x_scales = pack_weight(x, "e4m3")
    w_words, w_scales = pack4(w)
    return {
        "x_words": x_words, "x_scales": x_scales,
        "w_words": w_words, "w_scales": w_scales,
        "omega": bf(omega),
        "offset": bf(0.3 * np.random.randn(F)),
        "a": bf(np.exp(0.3 * np.random.randn(T)) * t),
        "b": bf(np.exp(0.3 * np.random.randn(T)) / np.sqrt(T) / t),
        "prev": bf(np.random.randn(F, L)),
        "gain": bf(np.exp(0.8 * np.random.randn(F))),
    }

def reference(x_words, x_scales, w_words, w_scales, omega, offset, a, b, prev, gain):
    XT = unpack_weight(x_words, x_scales, "e4m3")
    W = unpack4(w_words, w_scales)
    P = ((XT.T @ W) - f64(offset)) * f64(a)[:, None]
    S = (XT.T @ mxq(f64(omega), 0, "e4m3")) * f64(b)[:, None]
    Z = mxq(P, 0, "e4m3").T @ mxq(S, 0, "e4m3")
    y = (Z + f64(prev)) * f64(gain)[:, None]
    Y = y.reshape(F, L)
    words, scales = planes(Y)
    return y, words, scales

@@ -1,0 +1,459 @@
+from contextlib import ExitStack
+
+import concourse.mybir as mybir
+from concourse.masks import make_identity
+
+T, D, F, L = 2048, 1024, 1536, 256
+FLOPS = 2 * T * D * F + 2 * T * D * L + 2 * F * T * L
+
+F32 = mybir.dt.float32
+BF16 = mybir.dt.bfloat16
+I32 = mybir.dt.int32
+U32 = mybir.dt.uint32
+U8 = mybir.dt.uint8
+FP8X4 = mybir.dt.float8_e4m3fn_x4
+FP4X4 = mybir.dt.float4_e2m1fn_x4
+ALU = mybir.AluOpType
+COPY = mybir.ActivationFunctionType.Copy
+
+P = 128
+KP = 512
+NG = D // KP
+NC = T // KP
+NF = F // KP
+
+STEPS = [(0, 0), (1, 0), (0, 1), (0, 2), (0, 3), (1, 1), (1, 2), (1, 3), (2, 0), (2, 1), (2, 2), (2, 3)]
+ROUTES = "BBBBBBBBBBBB"
+
+
+def tile_range_finder_transposed_pass_k4_kernel(
+    tc, x_words, x_scales, w_words, w_scales, omega, offset, a, b, prev, gain, out_0, out_1, out_2
+):
+    nc = tc.nc
+    with ExitStack() as ctx:
+        keep = ctx.enter_context(tc.tile_pool(name="keep", bufs=1))
+        work = ctx.enter_context(tc.tile_pool(name="work", bufs=3))
+        psum = ctx.enter_context(tc.psum_pool(name="psum", bufs=1))
+        ctx.enter_context(tc.manual_schedule())
+
+        def kept(name, shape, dtype):
+            return keep.tile(shape, dtype, name=name, align_bytes=64)
+
+        x_raw = [kept("x_raw%d" % c, [P, NG, KP], U32) for c in range(NC)]
+        x_codes = [kept("x_codes%d" % c, [P, NG, KP], U32) for c in range(NC)]
+        xs_first = kept("xs_first", [P, NG, KP], U8)
+        xs_rest = kept("xs_rest", [P, NG, T - KP], U8)
+        x_sc = [kept("x_sc%d" % c, [P, NG, KP], U8) for c in range(NC)]
+        w_codes = [kept("w_codes%d" % g, [P, NG, 2 * KP], U8) for g in range(NF)]
+        w_sc = kept("w_sc", [P, NG, F], U8)
+        rows = kept("rows", [P, KP], BF16)
+        rows_b = kept("rows_b", [P, KP], BF16)
+        cols_bf = kept("cols_bf", [P, NC, 8], BF16)
+        cols_b = kept("cols_b", [P, NC, 8], F32)
+        off_wide = [kept("off_wide%d" % g, [P, KP], BF16) for g in range(NF)]
+        cols = kept("cols", [P, NC, 8], F32)
+        a_wide = [kept("a_wide%d" % c, [P, KP], BF16) for c in range(NC)]
+        gain_bf = kept("gain_bf", [P, NF, 4], BF16)
+        gain_f = kept("gain_f", [P, NF, 4], F32)
+        om_raw = kept("om_raw", [P, NG, 4, L], BF16)
+        om_grouped = kept("om_grouped", [P, NG, L, 4], BF16)
+        om_codes = kept("om_codes", [P, NG, L], U32)
+        om_sc = kept("om_sc", [P, NG, L], U8)
+        s_codes = [kept("s_codes%d" % c, [P, L], U32) for c in range(NC)]
+        s_sc = [kept("s_sc%d" % c, [P, L], U8) for c in range(NC)]
+        p_codes = {s: kept("p_codes%d_%d" % s, [P, KP], U32) for s in STEPS}
+        p_sc = {s: kept("p_sc%d_%d" % s, [P, KP], U8) for s in STEPS}
+        prev_raw = kept("prev_raw", [P, NF, 4, L], BF16)
+        prev_gain = [kept("prev_gain%d" % g, [P, 4, L], F32) for g in range(NF)]
+        y = [kept("y%d" % g, [P, 4, L], F32) for g in range(NF - 1)]
+        y_grouped = [kept("y_grouped%d" % g, [P, L, 4], BF16) for g in range(NF)]
+        y_codes = [kept("y_codes%d" % g, [P, L], U32) for g in range(NF)]
+        y_sc = [kept("y_sc%d" % g, [P, L], U8) for g in range(NF)]
+        ident_bf = kept("ident_bf", [P, P], BF16)
+        ident_f = kept("ident_f", [P, P], F32)
+
+        counts = {"acc": 0, "tr": 0, "z": 0}
+        depth = {"acc": 3, "tr": 3, "z": 2}
+
+        def bank(kind, shape, dtype):
+            tag = "%s%d" % (kind, counts[kind] % depth[kind])
+            counts[kind] += 1
+            return psum.tile(shape, dtype, name=tag, tag=tag)
+
+        def named_bank(tag, shape, dtype):
+            return psum.tile(shape, dtype, name=tag, tag=tag)
+
+        xw_view = x_words.rearrange("g p n t -> p g (n t)")
+        ww_view = w_words.rearrange("g p n -> p g n")
+        xs_view = x_scales.rearrange("g (Q r) n -> r Q g n", r=4)
+        ws_view = w_scales.rearrange("g (Q r) n -> r Q g n", r=4)
+
+        def load_x(c):
+            nc.sync.dma_start(out=x_raw[c][:].bitcast(I32), in_=xw_view[:, :, 4 * KP * c : 4 * KP * (c + 1)].bitcast(I32))
+
+        def load_w(g):
+            nc.sync.dma_start(out=w_codes[g][:].bitcast(I32), in_=ww_view[:, :, 2 * KP * g : 2 * KP * (g + 1)].bitcast(I32))
+
+        def load_scale_rows(queue, plane, view, r):
+            queue.dma_start(out=plane[r:P:32, :, :].bitcast(I32), in_=view.bitcast(I32))
+
+        def interleave(engine_copy, dst, src):
+            engine_copy(out=dst.rearrange("p (c i) t -> p c t i", i=4), in_=src.rearrange("p t (c i) -> p c t i", i=4))
+
+        def quantize(codes, scales, grouped):
+            nc.vector.quantize_mx(out=codes.bitcast(FP8X4), scales=scales, in_=grouped)
+
+        nc.vector.memset(rows[:], 0.0)
+        nc.vector.memset(xs_first[:].bitcast(I32), 0)
+        nc.vector.memset(w_sc[:].bitcast(I32), 0)
+        nc.vector.memset(rows_b[:], 0.0)
+        nc.vector.memset(xs_rest[:].bitcast(I32), 0)
+
+        make_identity(nc, ident_bf[:])
+        nc.sync.dma_start(
+            out=rows[4:8, 0 : NF * P].rearrange("f (g p) -> f g p", p=P), in_=offset.rearrange("(g f p) -> f g p", f=4, p=P)
+        )
+        nc.sync.dma_start(out=rows[0:4, :].rearrange("f (g p) -> f g p", p=P), in_=a.rearrange("(g f p) -> f g p", f=4, p=P))
+        load_x(0)
+        load_w(0)
+        for r in range(4):
+            load_scale_rows(nc.sync, xs_first, xs_view[r][:, :, 0:KP], r)
+        for r in range(4):
+            load_scale_rows(nc.sync if r < 2 else nc.gpsimd, w_sc, ws_view[r], r)
+        make_identity(nc, ident_f[:])
+        load_w(1)
+        load_x(1)
+        nc.sync.dma_start(out=rows_b[0:4, :].rearrange("j (m r) -> j m r", r=8), in_=b.rearrange("(m j r) -> j m r", j=4, r=8))
+        for r in range(4):
+            load_scale_rows(nc.sync, xs_rest, xs_view[r][:, :, KP:T], r)
+        nc.sync.dma_start(
+            out=om_raw[:].rearrange("p g t l -> p g (t l)"), in_=omega.rearrange("(g p t) l -> p g (t l)", p=P, t=4)
+        )
+        load_x(2)
+        load_x(3)
+        nc.sync.dma_start(out=gain_bf[:], in_=gain.rearrange("(g p t) -> p g t", p=P, t=4))
+        nc.sync.dma_start(
+            out=prev_raw[:].rearrange("p g t l -> p g (t l)"), in_=prev.rearrange("(g p t) l -> p g (t l)", p=P, t=4)
+        )
+        load_w(2)
+
+        def turn_rows(src, width, dst_bf, dst_f):
+            turned = bank("tr", [P, NC, P], BF16)
+            for c in range(NC):
+                nc.tensor.transpose(turned[:, c, :], src[:, P * c : P * (c + 1)], ident_bf[:])
+            if dst_bf is not None:
+                nc.scalar.activation(out=dst_bf[:], in_=turned[:, :, 0:width], func=COPY)
+            nc.scalar.copy(out=dst_f[:], in_=turned[:, :, 0:width])
+
+        def spread_offset(fg):
+            wide = bank("tr", [P, 4 * P], BF16)
+            for j in range(4):
+                nc.tensor.transpose(wide[:, P * j : P * (j + 1)], cols_bf[:, fg, 4 + j : 5 + j].to_broadcast([P, P]), ident_bf[:])
+            nc.scalar.copy(
+                out=off_wide[fg][:].rearrange("p (t m) -> p t m", t=4),
+                in_=wide[:].rearrange("p (m t) -> p t m", t=4),
+            )
+
+        def spread_a(c):
+            wide = bank("tr", [P, 4 * P], BF16)
+            for j in range(4):
+                nc.tensor.transpose(wide[:, P * j : P * (j + 1)], cols_bf[:, c, j : j + 1].to_broadcast([P, P]), ident_bf[:])
+            nc.scalar.copy(
+                out=a_wide[c][:].rearrange("p (u q r e) -> p u q r e", e=2, u=2, r=8),
+                in_=wide[:].rearrange("p (q e u r) -> p u q r e", e=2, u=2, r=8),
+            )
+
+        def permute_x(c):
+            nc.vector.tensor_copy(
+                out=x_codes[c][:].bitcast(I32).rearrange("p g (j q r) -> p g j q r", j=4, r=8),
+                in_=x_raw[c][:].bitcast(I32).rearrange("p g (q j r) -> p g j q r", j=4, r=8),
+            )
+            raw = xs_first[:] if c == 0 else xs_rest[:, :, KP * (c - 1) : KP * c]
+            nc.vector.tensor_copy(
+                out=x_sc[c][:].bitcast(I32).rearrange("p g (j q r) -> p g j q r", j=4, r=2),
+                in_=raw.bitcast(I32).rearrange("p g (q j r) -> p g j q r", j=4, r=2),
+            )
+
+        pt = {}
+        grouped = {}
+
+        def features(step, ft):
+            fg, c = step
+            if ft == 0:
+                pt[step] = work.tile([P, 4, KP], BF16, name="pt", tag="pt", align_bytes=64)
+            acc = bank("acc", [P, KP], F32)
+            for g in range(NG):
+                nc.tensor.matmul_mx(
+                    out=acc[:],
+                    lhsT=w_codes[fg][:, g, 2 * P * ft : 2 * P * (ft + 1)].bitcast(FP4X4),
+                    lhsT_scale=w_sc[:, g, KP * fg + P * ft : KP * fg + P * (ft + 1)],
+                    rhs=x_codes[c][:, g, :].bitcast(FP8X4),
+                    rhs_scale=x_sc[c][:, g, :],
+                    start=(g == 0),
+                    stop=(g == NG - 1),
+                )
+            nc.vector.scalar_tensor_tensor(
+                out=pt[step][:, ft, :].rearrange("p (w e) -> p w e", e=2),
+                in0=acc[:].rearrange("p (e w) -> p w e", e=2),
+                scalar=cols[:, fg, 4 + ft : 5 + ft],
+                in1=a_wide[c][:].rearrange("p (w e) -> p w e", e=2),
+                op0=ALU.subtract,
+                op1=ALU.mult,
+            )
+
+        def turn(step, h, engine_copy):
+            if h == 0:
+                grouped[step] = work.tile([P, 4 * KP], BF16, name="grouped", tag="grouped", align_bytes=64)
+            tr = bank("tr", [P, 2, 2 * P], F32)
+            for i in range(2):
+                words = pt[step][:, 2 * h + i, :].bitcast(F32)
+                for u in range(2):
+                    nc.tensor.transpose(tr[:, u, P * i : P * (i + 1)], words[:, P * u : P * (u + 1)], ident_f[:])
+            dst = grouped[step][:].bitcast(F32).rearrange("p (t h m u) -> p t h m u", t=4, h=2, u=2)[:, :, h, :, :]
+            engine_copy(out=dst, in_=tr[:].rearrange("p u (m t) -> p t m u", t=4))
+
+        shifts = {}
+
+        def make_shift(step, j):
+            fg, c = step
+            shifts[(step, j)] = work.tile([P, KP], F32, name="shift", tag="shift", align_bytes=64, bufs=4)
+            nc.gpsimd.tensor_scalar(
+                out=shifts[(step, j)][:], in0=off_wide[fg][:], scalar1=cols_b[:, c, 4 + j : 5 + j], scalar2=0.0, op0=ALU.mult, op1=ALU.add
+            )
+
+        def tokens(step, j):
+            fg, c = step
+            if j == 0:
+                pt[step] = work.tile([P, 4, KP], BF16, name="pt", tag="pt", align_bytes=64)
+            acc = bank("acc", [P, KP], F32)
+            for g in range(NG):
+                nc.tensor.matmul_mx(
+                    out=acc[:],
+                    lhsT=x_codes[c][:, g, P * j : P * (j + 1)].bitcast(FP8X4),
+                    lhsT_scale=x_sc[c][:, g, P * j : P * (j + 1)],
+                    rhs=w_codes[fg][:, g, :].bitcast(FP4X4),
+                    rhs_scale=w_sc[:, g, KP * fg : KP * (fg + 1)],
+                    start=(g == 0),
+                    stop=(g == NG - 1),
+                )
+            e, u = divmod(j, 2)
+            nc.vector.scalar_tensor_tensor(
+                out=pt[step][:, 2 * u + e, :].rearrange("p (t m) -> p t m", t=4),
+                in0=acc[:].rearrange("p (m t) -> p t m", t=4),
+                scalar=cols_b[:, c, 4 + j : 5 + j],
+                in1=shifts[(step, j)][:].rearrange("p (t m) -> p t m", t=4),
+                op0=ALU.mult,
+                op1=ALU.subtract,
+            )
+
+        def weave(step, engine_copy, lo, hi):
+            if lo == 0:
+                grouped[step] = work.tile([P, 4 * KP], BF16, name="grouped", tag="grouped", align_bytes=64)
+            interleave(engine_copy, grouped[step][:].rearrange("p (f t) -> p f t", t=4)[:, lo:hi, :], pt[step][:, :, lo:hi])
+
+        def turn_one(step, ft, engine_copy):
+            if ft == 0:
+                grouped[step] = work.tile([P, 4 * KP], BF16, name="grouped", tag="grouped", align_bytes=64)
+            tr = bank("tr", [P, 2, P], F32)
+            words = pt[step][:, ft, :].bitcast(F32)
+            for u in range(2):
+                nc.tensor.transpose(tr[:, u, :], words[:, P * u : P * (u + 1)], ident_f[:])
+            dst = grouped[step][:].bitcast(F32).rearrange("p (t h m u) -> p t h m u", t=4, h=4, u=2)[:, :, ft, :, :]
+            engine_copy(out=dst, in_=tr[:].rearrange("p u (m t) -> p t m u", t=4))
+
+        def quantize_p(step):
+            quantize(p_codes[step][:], p_sc[step][:], grouped[step][:])
+
+        def prepare_omega():
+            for g in range(NG):
+                interleave(nc.scalar.copy, om_grouped[:, g, :, :], om_raw[:, g, :, :])
+
+        def quantize_omega():
+            quantize(
+                om_codes[:].rearrange("p g l -> p (g l)"),
+                om_sc[:].rearrange("p g l -> p (g l)"),
+                om_grouped[:].rearrange("p g l t -> p (g l t)"),
+            )
+
+        s_grouped = {}
+        s_banks = {}
+
+        def sketch(c):
+            for e in range(2):
+                acc = bank("z", [P, 2, L], F32)
+                s_banks[(c, e)] = acc
+                for u in range(2):
+                    j = 2 * e + u
+                    for g in range(NG):
+                        nc.tensor.matmul_mx(
+                            out=acc[:, u, :],
+                            lhsT=x_codes[c][:, g, P * j : P * (j + 1)].bitcast(FP8X4),
+                            lhsT_scale=x_sc[c][:, g, P * j : P * (j + 1)],
+                            rhs=om_codes[:, g, :].bitcast(FP8X4),
+                            rhs_scale=om_sc[:, g, :],
+                            start=(g == 0),
+                            stop=(g == NG - 1),
+                        )
+
+        def weigh_sketch(c):
+            s_rows = work.tile([P, 4, L], BF16, name="s_rows", tag="s_rows", align_bytes=64)
+            for e in range(2):
+                acc = s_banks[(c, e)]
+                for u in range(2):
+                    j = 2 * e + u
+                    nc.scalar.activation(out=s_rows[:, 2 * u + e, :], in_=acc[:, u, :], func=COPY, scale=cols_b[:, c, j : j + 1])
+            s_grouped[c] = work.tile([P, L, 4], BF16, name="s_grouped", tag="s_grouped", align_bytes=64)
+            interleave(nc.scalar.copy, s_grouped[c][:], s_rows[:])
+
+        def quantize_s(c):
+            quantize(s_codes[c][:], s_sc[c][:], s_grouped[c][:].rearrange("p l t -> p (l t)"))
+
+        def scale_prev(fg):
+            for t in range(4):
+                nc.scalar.activation(out=prev_gain[fg][:, t, :], in_=prev_raw[:, fg, t, :], func=COPY, scale=gain_f[:, fg, t : t + 1])
+
+        def cross_pass(acc, fg, t, c, k):
+            nc.tensor.matmul_mx(
+                out=acc,
+                lhsT=p_codes[(fg, c)][:, P * t : P * (t + 1)].bitcast(FP8X4),
+                lhsT_scale=p_sc[(fg, c)][:, P * t : P * (t + 1)],
+                rhs=s_codes[c][:].bitcast(FP8X4),
+                rhs_scale=s_sc[c][:],
+                start=(k == 0),
+                stop=(k == NC - 1),
+            )
+
+        def finish(acc, fg, t):
+            nc.vector.scalar_tensor_tensor(
+                out=y[fg][:, t, :], in0=acc, scalar=gain_f[:, fg, t : t + 1], in1=prev_gain[fg][:, t, :], op0=ALU.mult, op1=ALU.add
+            )
+
+        z_banks = {}
+
+        def cross_pair(fg, h):
+            acc = bank("z", [P, 2, L], F32)
+            for i in range(2):
+                for c in range(NC):
+                    cross_pass(acc[:, i, :], fg, 2 * h + i, c, c)
+            z_banks[(fg, h)] = acc
+
+        def finish_pair(fg, h):
+            for i in range(2):
+                finish(z_banks[(fg, h)][:, i, :], fg, 2 * h + i)
+
+        def store_y(fg):
+            nc.sync.dma_start(
+                out=out_0[KP * fg : KP * (fg + 1), :].rearrange("(p t) l -> p (t l)", t=4), in_=y[fg][:].rearrange("p t l -> p (t l)")
+            )
+
+        def planes(fg):
+            quantize(y_codes[fg][:], y_sc[fg][:], y_grouped[fg][:].rearrange("p l t -> p (l t)"))
+            store_planes(fg)
+
+        def store_planes(fg):
+            nc.sync.dma_start(out=out_1[fg].rearrange("p l t -> p (l t)").bitcast(I32), in_=y_codes[fg][:].bitcast(I32))
+            rows_out = out_2[fg].rearrange("(Q r) l -> r Q l", r=4)
+            for r in range(4):
+                nc.sync.dma_start(out=rows_out[r].bitcast(I32), in_=y_sc[fg][r:P:32, :].bitcast(I32))
+
+        turn_rows(rows, 8, cols_bf, cols)
+        for c in range(NC):
+            spread_a(c)
+        permute_x(0)
+
+        last = len(STEPS) - 1
+        tail = STEPS[last]
+        for s, step in enumerate(STEPS[:last]):
+            for ft in range(4):
+                features(step, ft)
+            if 2 <= s <= 5:
+                sketch(s - 2)
+            if s in (7, 8):
+                cross_pair(0, s - 7)
+            if s == 10:
+                cross_pair(1, 0)
+                cross_pair(1, 1)
+            if s >= 1:
+                for h in range(2):
+                    turn(STEPS[s - 1], h, nc.scalar.copy)
+            if s == 1:
+                turn_rows(rows_b, 8, None, cols_b)
+            if 2 <= s <= 5:
+                weigh_sketch(s - 2)
+            if s == 0:
+                prepare_omega()
+                permute_x(1)
+            if s == 1:
+                quantize_omega()
+            if s == 2:
+                permute_x(2)
+            if s == 3:
+                permute_x(3)
+                nc.scalar.copy(out=gain_f[:], in_=gain_bf[:])
+            if s >= 2:
+                quantize_p(STEPS[s - 2])
+            if 3 <= s <= 6:
+                quantize_s(s - 3)
+            if s in (6, 7, 8):
+                scale_prev(s - 6)
+            if s in (7, 8):
+                finish_pair(0, s - 7)
+            if s == 8:
+                store_y(0)
+                interleave(nc.scalar.copy, y_grouped[0][:], y[0][:])
+            if s == 9:
+                planes(0)
+            if s == 10:
+                finish_pair(1, 0)
+                finish_pair(1, 1)
+
+        fg = NF - 1
+        order = [c for (g, c) in STEPS if g == fg]
+        open_banks = {}
+
+        def tail_pass(t, k):
+            if k == 0:
+                open_banks[t] = named_bank(("z0", "z1", "acc0", "acc1")[t], [P, L], F32)
+            cross_pass(open_banks[t][:], fg, t, order[k], k)
+
+        store_y(1)
+        features(tail, 0)
+        features(tail, 1)
+        for h in range(2):
+            turn(STEPS[last - 1], h, nc.scalar.copy)
+        interleave(nc.scalar.copy, y_grouped[1][:], y[1][:])
+        quantize_p(STEPS[last - 2])
+        features(tail, 2)
+        features(tail, 3)
+        for k in range(2):
+            for t in range(2):
+                tail_pass(t, k)
+        for ft in range(3):
+            turn_one(tail, ft, nc.scalar.copy)
+        quantize_p(STEPS[last - 1])
+        planes(1)
+        turn_one(tail, 3, nc.scalar.copy)
+        for t, k in ((0, 2), (1, 2), (2, 0), (3, 0), (2, 1), (3, 1), (2, 2), (3, 2)):
+            tail_pass(t, k)
+        for t in range(4):
+            quantize(
+                p_codes[tail][:, P * t : P * (t + 1)], p_sc[tail][:, P * t : P * (t + 1)], grouped[tail][:, KP * t : KP * (t + 1)]
+            )
+        for t in range(4):
+            tail_pass(t, NC - 1)
+        half = L // 2
+        y_half = [kept("y_half%d" % h, [P, 4, half], F32) for h in range(2)]
+        out_rows = out_0[KP * fg : KP * (fg + 1), :].rearrange("(p t) l -> p t l", t=4)
+        for h in range(2):
+            ls = slice(half * h, half * (h + 1))
+            for t in range(4):
+                nc.vector.scalar_tensor_tensor(
+                    out=y_half[h][:, t, :], in0=open_banks[t][:, ls], scalar=gain_f[:, fg, t : t + 1], in1=prev_gain[fg][:, t, ls],
+                    op0=ALU.mult, op1=ALU.add,
+                )
+            nc.sync.dma_start(out=out_rows[:, :, ls], in_=y_half[h][:])
+            interleave(nc.scalar.copy if h == 0 else nc.vector.tensor_copy, y_grouped[fg][:, ls, :], y_half[h][:])
+        for h in range(2):
+            ls = slice(half * h, half * (h + 1))
+            quantize(y_codes[fg][:, ls], y_sc[fg][:, ls], y_grouped[fg][:, ls, :].rearrange("p l t -> p (l t)"))
+        store_planes(fg)

@@ -21,9 +21,7 @@ KP = 512
 NG = D // KP
 NC = T // KP
 NF = F // KP
-
-STEPS = [(0, 0), (1, 0), (0, 1), (0, 2), (0, 3), (1, 1), (1, 2), (1, 3), (2, 0), (2, 1), (2, 2), (2, 3)]
-ROUTES = "BBBBBBBBBBBB"
+ALIGN = 256
 
 
 def tile_range_finder_transposed_pass_k4_kernel(
@@ -37,32 +35,38 @@ def tile_range_finder_transposed_pass_k4_kernel(
         ctx.enter_context(tc.manual_schedule())
 
         def kept(name, shape, dtype):
-            return keep.tile(shape, dtype, name=name, align_bytes=64)
+            return keep.tile(shape, dtype, name=name, align_bytes=ALIGN)
 
+        def passing(name, shape, dtype, bufs):
+            return work.tile(shape, dtype, name=name, tag=name, align_bytes=ALIGN, bufs=bufs)
+
+        blocks = [(fg, c) for fg in range(NF) for c in range(NC)]
         x_raw = [kept("x_raw%d" % c, [P, NG, KP], U32) for c in range(NC)]
         x_codes = [kept("x_codes%d" % c, [P, NG, KP], U32) for c in range(NC)]
         xs_first = kept("xs_first", [P, NG, KP], U8)
         xs_rest = kept("xs_rest", [P, NG, T - KP], U8)
         x_sc = [kept("x_sc%d" % c, [P, NG, KP], U8) for c in range(NC)]
         w_codes = [kept("w_codes%d" % g, [P, NG, 2 * KP], U8) for g in range(NF)]
-        w_sc = kept("w_sc", [P, NG, F], U8)
+        ws_first = kept("ws_first", [P, NG, KP], U8)
+        ws_rest = kept("ws_rest", [P, NG, F - KP], U8)
+        w_sc = [ws_first[:]] + [ws_rest[:, :, KP * g : KP * (g + 1)] for g in range(NF - 1)]
         rows = kept("rows", [P, KP], BF16)
         rows_b = kept("rows_b", [P, KP], BF16)
         cols_bf = kept("cols_bf", [P, NC, 8], BF16)
+        cols = kept("cols", [P, NC, 4], F32)
         cols_b = kept("cols_b", [P, NC, 8], F32)
-        off_wide = [kept("off_wide%d" % g, [P, KP], BF16) for g in range(NF)]
-        cols = kept("cols", [P, NC, 8], F32)
-        a_wide = [kept("a_wide%d" % c, [P, KP], BF16) for c in range(NC)]
+        off_first = kept("off_first", [P, KP], BF16)
+        off_rest = kept("off_rest", [P, F - KP], BF16)
+        a_wide = {c: kept("a_wide%d" % c, [P, KP], BF16) for c in (0, 2, 3)}
         gain_bf = kept("gain_bf", [P, NF, 4], BF16)
-        gain_f = kept("gain_f", [P, NF, 4], F32)
         om_raw = kept("om_raw", [P, NG, 4, L], BF16)
         om_grouped = kept("om_grouped", [P, NG, L, 4], BF16)
         om_codes = kept("om_codes", [P, NG, L], U32)
         om_sc = kept("om_sc", [P, NG, L], U8)
         s_codes = [kept("s_codes%d" % c, [P, L], U32) for c in range(NC)]
         s_sc = [kept("s_sc%d" % c, [P, L], U8) for c in range(NC)]
-        p_codes = {s: kept("p_codes%d_%d" % s, [P, KP], U32) for s in STEPS}
-        p_sc = {s: kept("p_sc%d_%d" % s, [P, KP], U8) for s in STEPS}
+        p_codes = {s: kept("p_codes%d_%d" % s, [P, KP], U32) for s in blocks}
+        p_sc = {s: kept("p_sc%d_%d" % s, [P, KP], U8) for s in blocks}
         prev_raw = kept("prev_raw", [P, NF, 4, L], BF16)
         prev_gain = [kept("prev_gain%d" % g, [P, 4, L], F32) for g in range(NF)]
         y = [kept("y%d" % g, [P, 4, L], F32) for g in range(NF - 1)]
@@ -75,27 +79,37 @@ def tile_range_finder_transposed_pass_k4_kernel(
         counts = {"acc": 0, "tr": 0, "z": 0}
         depth = {"acc": 3, "tr": 3, "z": 2}
 
+        def named_bank(tag, shape, dtype):
+            return psum.tile(shape, dtype, name=tag, tag=tag)
+
         def bank(kind, shape, dtype):
             tag = "%s%d" % (kind, counts[kind] % depth[kind])
             counts[kind] += 1
-            return psum.tile(shape, dtype, name=tag, tag=tag)
-
-        def named_bank(tag, shape, dtype):
-            return psum.tile(shape, dtype, name=tag, tag=tag)
+            return named_bank(tag, shape, dtype)
 
         xw_view = x_words.rearrange("g p n t -> p g (n t)")
         ww_view = w_words.rearrange("g p n -> p g n")
         xs_view = x_scales.rearrange("g (Q r) n -> r Q g n", r=4)
         ws_view = w_scales.rearrange("g (Q r) n -> r Q g n", r=4)
 
-        def load_x(c):
-            nc.sync.dma_start(out=x_raw[c][:].bitcast(I32), in_=xw_view[:, :, 4 * KP * c : 4 * KP * (c + 1)].bitcast(I32))
+        def load_x(queue, c):
+            queue.dma_start(out=x_raw[c][:].bitcast(I32), in_=xw_view[:, :, 4 * KP * c : 4 * KP * (c + 1)].bitcast(I32))
 
-        def load_w(g):
-            nc.sync.dma_start(out=w_codes[g][:].bitcast(I32), in_=ww_view[:, :, 2 * KP * g : 2 * KP * (g + 1)].bitcast(I32))
+        def load_w(queue, g):
+            queue.dma_start(out=w_codes[g][:].bitcast(I32), in_=ww_view[:, :, 2 * KP * g : 2 * KP * (g + 1)].bitcast(I32))
 
-        def load_scale_rows(queue, plane, view, r):
-            queue.dma_start(out=plane[r:P:32, :, :].bitcast(I32), in_=view.bitcast(I32))
+        def load_scale_rows(plane, view, lo, hi):
+            for r in range(4):
+                nc.sync.dma_start(out=plane[r:P:32, :, :].bitcast(I32), in_=view[r][:, :, lo:hi].bitcast(I32))
+
+        def load_slices(dst, vec):
+            nc.sync.dma_start(out=dst.rearrange("j (m r) -> j m r", r=8), in_=vec.rearrange("(m j r) -> j m r", j=4, r=8))
+
+        def load_tiles(dst, vec):
+            nc.sync.dma_start(out=dst.rearrange("f (g p) -> f g p", p=P), in_=vec.rearrange("(g f p) -> f g p", f=4, p=P))
+
+        def load_grouped_rows(dst, mat):
+            nc.sync.dma_start(out=dst.rearrange("p g t l -> p g (t l)"), in_=mat.rearrange("(g p t) l -> p g (t l)", p=P, t=4))
 
         def interleave(engine_copy, dst, src):
             engine_copy(out=dst.rearrange("p (c i) t -> p c t i", i=4), in_=src.rearrange("p t (c i) -> p c t i", i=4))
@@ -103,64 +117,23 @@ def tile_range_finder_transposed_pass_k4_kernel(
         def quantize(codes, scales, grouped):
             nc.vector.quantize_mx(out=codes.bitcast(FP8X4), scales=scales, in_=grouped)
 
-        nc.vector.memset(rows[:], 0.0)
-        nc.vector.memset(xs_first[:].bitcast(I32), 0)
-        nc.vector.memset(w_sc[:].bitcast(I32), 0)
-        nc.vector.memset(rows_b[:], 0.0)
-        nc.vector.memset(xs_rest[:].bitcast(I32), 0)
-
-        make_identity(nc, ident_bf[:])
-        nc.sync.dma_start(
-            out=rows[4:8, 0 : NF * P].rearrange("f (g p) -> f g p", p=P), in_=offset.rearrange("(g f p) -> f g p", f=4, p=P)
-        )
-        nc.sync.dma_start(out=rows[0:4, :].rearrange("f (g p) -> f g p", p=P), in_=a.rearrange("(g f p) -> f g p", f=4, p=P))
-        load_x(0)
-        load_w(0)
-        for r in range(4):
-            load_scale_rows(nc.sync, xs_first, xs_view[r][:, :, 0:KP], r)
-        for r in range(4):
-            load_scale_rows(nc.sync if r < 2 else nc.gpsimd, w_sc, ws_view[r], r)
-        make_identity(nc, ident_f[:])
-        load_w(1)
-        load_x(1)
-        nc.sync.dma_start(out=rows_b[0:4, :].rearrange("j (m r) -> j m r", r=8), in_=b.rearrange("(m j r) -> j m r", j=4, r=8))
-        for r in range(4):
-            load_scale_rows(nc.sync, xs_rest, xs_view[r][:, :, KP:T], r)
-        nc.sync.dma_start(
-            out=om_raw[:].rearrange("p g t l -> p g (t l)"), in_=omega.rearrange("(g p t) l -> p g (t l)", p=P, t=4)
-        )
-        load_x(2)
-        load_x(3)
-        nc.sync.dma_start(out=gain_bf[:], in_=gain.rearrange("(g p t) -> p g t", p=P, t=4))
-        nc.sync.dma_start(
-            out=prev_raw[:].rearrange("p g t l -> p g (t l)"), in_=prev.rearrange("(g p t) l -> p g (t l)", p=P, t=4)
-        )
-        load_w(2)
-
-        def turn_rows(src, width, dst_bf, dst_f):
+        def turn_rows(src):
             turned = bank("tr", [P, NC, P], BF16)
             for c in range(NC):
                 nc.tensor.transpose(turned[:, c, :], src[:, P * c : P * (c + 1)], ident_bf[:])
-            if dst_bf is not None:
-                nc.scalar.activation(out=dst_bf[:], in_=turned[:, :, 0:width], func=COPY)
-            nc.scalar.copy(out=dst_f[:], in_=turned[:, :, 0:width])
+            return turned
 
-        def spread_offset(fg):
+        def spread(block, first):
             wide = bank("tr", [P, 4 * P], BF16)
             for j in range(4):
-                nc.tensor.transpose(wide[:, P * j : P * (j + 1)], cols_bf[:, fg, 4 + j : 5 + j].to_broadcast([P, P]), ident_bf[:])
-            nc.scalar.copy(
-                out=off_wide[fg][:].rearrange("p (t m) -> p t m", t=4),
-                in_=wide[:].rearrange("p (m t) -> p t m", t=4),
-            )
+                column = cols_bf[:, block, first + j : first + j + 1]
+                nc.tensor.transpose(wide[:, P * j : P * (j + 1)], column.to_broadcast([P, P]), ident_bf[:])
+            return wide
 
-        def spread_a(c):
-            wide = bank("tr", [P, 4 * P], BF16)
-            for j in range(4):
-                nc.tensor.transpose(wide[:, P * j : P * (j + 1)], cols_bf[:, c, j : j + 1].to_broadcast([P, P]), ident_bf[:])
-            nc.scalar.copy(
+        def spread_a(c, engine_copy):
+            engine_copy(
                 out=a_wide[c][:].rearrange("p (u q r e) -> p u q r e", e=2, u=2, r=8),
-                in_=wide[:].rearrange("p (q e u r) -> p u q r e", e=2, u=2, r=8),
+                in_=spread(c, 0)[:].rearrange("p (q e u r) -> p u q r e", e=2, u=2, r=8),
             )
 
         def permute_x(c):
@@ -176,17 +149,18 @@ def tile_range_finder_transposed_pass_k4_kernel(
 
         pt = {}
         grouped = {}
+        shifts = {}
 
         def features(step, ft):
             fg, c = step
             if ft == 0:
-                pt[step] = work.tile([P, 4, KP], BF16, name="pt", tag="pt", align_bytes=64)
+                pt[step] = passing("pt", [P, 4, KP], BF16, 3)
             acc = bank("acc", [P, KP], F32)
             for g in range(NG):
                 nc.tensor.matmul_mx(
                     out=acc[:],
                     lhsT=w_codes[fg][:, g, 2 * P * ft : 2 * P * (ft + 1)].bitcast(FP4X4),
-                    lhsT_scale=w_sc[:, g, KP * fg + P * ft : KP * fg + P * (ft + 1)],
+                    lhsT_scale=w_sc[fg][:, g, P * ft : P * (ft + 1)],
                     rhs=x_codes[c][:, g, :].bitcast(FP8X4),
                     rhs_scale=x_sc[c][:, g, :],
                     start=(g == 0),
@@ -195,36 +169,44 @@ def tile_range_finder_transposed_pass_k4_kernel(
             nc.vector.scalar_tensor_tensor(
                 out=pt[step][:, ft, :].rearrange("p (w e) -> p w e", e=2),
                 in0=acc[:].rearrange("p (e w) -> p w e", e=2),
-                scalar=cols[:, fg, 4 + ft : 5 + ft],
+                scalar=cols[:, fg, ft : ft + 1],
                 in1=a_wide[c][:].rearrange("p (w e) -> p w e", e=2),
                 op0=ALU.subtract,
                 op1=ALU.mult,
             )
 
-        def turn(step, h, engine_copy):
-            if h == 0:
-                grouped[step] = work.tile([P, 4 * KP], BF16, name="grouped", tag="grouped", align_bytes=64)
-            tr = bank("tr", [P, 2, 2 * P], F32)
-            for i in range(2):
-                words = pt[step][:, 2 * h + i, :].bitcast(F32)
+        def turn(step, first, count, engine_copy):
+            if first == 0:
+                grouped[step] = passing("grouped", [P, 4 * KP], BF16, 4)
+            tr = bank("tr", [P, 2, count * P], F32)
+            for i in range(count):
+                words = pt[step][:, first + i, :].bitcast(F32)
                 for u in range(2):
                     nc.tensor.transpose(tr[:, u, P * i : P * (i + 1)], words[:, P * u : P * (u + 1)], ident_f[:])
-            dst = grouped[step][:].bitcast(F32).rearrange("p (t h m u) -> p t h m u", t=4, h=2, u=2)[:, :, h, :, :]
+            dst = grouped[step][:].bitcast(F32).rearrange("p (t m u) -> p t m u", t=4, u=2)[:, :, 32 * first : 32 * (first + count), :]
             engine_copy(out=dst, in_=tr[:].rearrange("p u (m t) -> p t m u", t=4))
 
-        shifts = {}
+        def turn_all(step):
+            for first in (0, 2):
+                turn(step, first, 2, nc.scalar.copy)
 
         def make_shift(step, j):
             fg, c = step
-            shifts[(step, j)] = work.tile([P, KP], F32, name="shift", tag="shift", align_bytes=64, bufs=4)
+            shifts[(step, j)] = passing("shift", [P, KP], F32, 4)
+            off = off_first[:] if fg == 0 else off_rest[:, KP * (fg - 1) : KP * fg]
             nc.gpsimd.tensor_scalar(
-                out=shifts[(step, j)][:], in0=off_wide[fg][:], scalar1=cols_b[:, c, 4 + j : 5 + j], scalar2=0.0, op0=ALU.mult, op1=ALU.add
+                out=shifts[(step, j)][:].rearrange("p (t m) -> p t m", t=4),
+                in0=off.rearrange("p (m t) -> p t m", t=4),
+                scalar1=cols_b[:, c, 4 + j : 5 + j],
+                scalar2=0.0,
+                op0=ALU.mult,
+                op1=ALU.add,
             )
 
         def tokens(step, j):
             fg, c = step
             if j == 0:
-                pt[step] = work.tile([P, 4, KP], BF16, name="pt", tag="pt", align_bytes=64)
+                pt[step] = passing("pt", [P, 4, KP], BF16, 3)
             acc = bank("acc", [P, KP], F32)
             for g in range(NG):
                 nc.tensor.matmul_mx(
@@ -232,7 +214,7 @@ def tile_range_finder_transposed_pass_k4_kernel(
                     lhsT=x_codes[c][:, g, P * j : P * (j + 1)].bitcast(FP8X4),
                     lhsT_scale=x_sc[c][:, g, P * j : P * (j + 1)],
                     rhs=w_codes[fg][:, g, :].bitcast(FP4X4),
-                    rhs_scale=w_sc[:, g, KP * fg : KP * (fg + 1)],
+                    rhs_scale=w_sc[fg][:, g, :],
                     start=(g == 0),
                     stop=(g == NG - 1),
                 )
@@ -246,20 +228,20 @@ def tile_range_finder_transposed_pass_k4_kernel(
                 op1=ALU.subtract,
             )
 
-        def weave(step, engine_copy, lo, hi):
+        def weave(step, lo, hi, engine_copy):
             if lo == 0:
-                grouped[step] = work.tile([P, 4 * KP], BF16, name="grouped", tag="grouped", align_bytes=64)
+                grouped[step] = passing("grouped", [P, 4 * KP], BF16, 4)
             interleave(engine_copy, grouped[step][:].rearrange("p (f t) -> p f t", t=4)[:, lo:hi, :], pt[step][:, :, lo:hi])
 
-        def turn_one(step, ft, engine_copy):
-            if ft == 0:
-                grouped[step] = work.tile([P, 4 * KP], BF16, name="grouped", tag="grouped", align_bytes=64)
-            tr = bank("tr", [P, 2, P], F32)
-            words = pt[step][:, ft, :].bitcast(F32)
-            for u in range(2):
-                nc.tensor.transpose(tr[:, u, :], words[:, P * u : P * (u + 1)], ident_f[:])
-            dst = grouped[step][:].bitcast(F32).rearrange("p (t h m u) -> p t h m u", t=4, h=4, u=2)[:, :, ft, :, :]
-            engine_copy(out=dst, in_=tr[:].rearrange("p u (m t) -> p t m u", t=4))
+        def by_features(step):
+            for ft in range(4):
+                features(step, ft)
+
+        def by_tokens(step, following):
+            for j in range(4):
+                tokens(step, j)
+                if following is not None:
+                    make_shift(following, j)
 
         def quantize_p(step):
             quantize(p_codes[step][:], p_sc[step][:], grouped[step][:])
@@ -295,22 +277,31 @@ def tile_range_finder_transposed_pass_k4_kernel(
                             stop=(g == NG - 1),
                         )
 
+        s_rows = {}
+
         def weigh_sketch(c):
-            s_rows = work.tile([P, 4, L], BF16, name="s_rows", tag="s_rows", align_bytes=64)
+            s_rows[c] = passing("s_rows", [P, 4, L], BF16, 3)
             for e in range(2):
-                acc = s_banks[(c, e)]
                 for u in range(2):
                     j = 2 * e + u
-                    nc.scalar.activation(out=s_rows[:, 2 * u + e, :], in_=acc[:, u, :], func=COPY, scale=cols_b[:, c, j : j + 1])
-            s_grouped[c] = work.tile([P, L, 4], BF16, name="s_grouped", tag="s_grouped", align_bytes=64)
-            interleave(nc.scalar.copy, s_grouped[c][:], s_rows[:])
+                    nc.scalar.activation(
+                        out=s_rows[c][:, 2 * u + e, :], in_=s_banks[(c, e)][:, u, :], func=COPY, scale=cols_b[:, c, j : j + 1]
+                    )
+
+        def weave_sketch(c):
+            s_grouped[c] = passing("s_grouped", [P, L, 4], BF16, 4)
+            interleave(nc.scalar.copy, s_grouped[c][:], s_rows[c][:])
 
         def quantize_s(c):
             quantize(s_codes[c][:], s_sc[c][:], s_grouped[c][:].rearrange("p l t -> p (l t)"))
 
-        def scale_prev(fg):
-            for t in range(4):
-                nc.scalar.activation(out=prev_gain[fg][:, t, :], in_=prev_raw[:, fg, t, :], func=COPY, scale=gain_f[:, fg, t : t + 1])
+        def scale_prev(first, count):
+            for n in range(first, first + count):
+                fg, t = divmod(n, 4)
+                nc.gpsimd.tensor_scalar(
+                    out=prev_gain[fg][:, t, :], in0=prev_raw[:, fg, t, :], scalar1=gain_bf[:, fg, t : t + 1], scalar2=0.0,
+                    op0=ALU.mult, op1=ALU.add,
+                )
 
         def cross_pass(acc, fg, t, c, k):
             nc.tensor.matmul_mx(
@@ -323,11 +314,6 @@ def tile_range_finder_transposed_pass_k4_kernel(
                 stop=(k == NC - 1),
             )
 
-        def finish(acc, fg, t):
-            nc.vector.scalar_tensor_tensor(
-                out=y[fg][:, t, :], in0=acc, scalar=gain_f[:, fg, t : t + 1], in1=prev_gain[fg][:, t, :], op0=ALU.mult, op1=ALU.add
-            )
-
         z_banks = {}
 
         def cross_pair(fg, h):
@@ -337,123 +323,278 @@ def tile_range_finder_transposed_pass_k4_kernel(
                     cross_pass(acc[:, i, :], fg, 2 * h + i, c, c)
             z_banks[(fg, h)] = acc
 
-        def finish_pair(fg, h):
-            for i in range(2):
-                finish(z_banks[(fg, h)][:, i, :], fg, 2 * h + i)
-
-        def store_y(fg):
-            nc.sync.dma_start(
-                out=out_0[KP * fg : KP * (fg + 1), :].rearrange("(p t) l -> p (t l)", t=4), in_=y[fg][:].rearrange("p t l -> p (t l)")
+        def finish(dst, acc, fg, t, ls):
+            nc.vector.scalar_tensor_tensor(
+                out=dst, in0=acc, scalar=gain_bf[:, fg, t : t + 1], in1=prev_gain[fg][:, t, ls], op0=ALU.mult, op1=ALU.add
             )
 
-        def planes(fg):
-            quantize(y_codes[fg][:], y_sc[fg][:], y_grouped[fg][:].rearrange("p l t -> p (l t)"))
-            store_planes(fg)
+        def finish_pair(fg, h):
+            for i in range(2):
+                t = 2 * h + i
+                finish(y[fg][:, t, :], z_banks[(fg, h)][:, i, :], fg, t, slice(0, L))
 
-        def store_planes(fg):
+        def out_rows(fg):
+            return out_0[KP * fg : KP * (fg + 1), :].rearrange("(p t) l -> p t l", t=4)
+
+        def store_y(fg):
+            nc.sync.dma_start(out=out_rows(fg).rearrange("p t l -> p (t l)"), in_=y[fg][:].rearrange("p t l -> p (t l)"))
+
+        def weave_y(fg):
+            interleave(nc.scalar.copy, y_grouped[fg][:], y[fg][:])
+
+        def store_planes(fg, second_queue):
             nc.sync.dma_start(out=out_1[fg].rearrange("p l t -> p (l t)").bitcast(I32), in_=y_codes[fg][:].bitcast(I32))
             rows_out = out_2[fg].rearrange("(Q r) l -> r Q l", r=4)
             for r in range(4):
-                nc.sync.dma_start(out=rows_out[r].bitcast(I32), in_=y_sc[fg][r:P:32, :].bitcast(I32))
+                queue = second_queue if r % 2 else nc.sync
+                queue.dma_start(out=rows_out[r].bitcast(I32), in_=y_sc[fg][r:P:32, :].bitcast(I32))
 
-        turn_rows(rows, 8, cols_bf, cols)
-        for c in range(NC):
-            spread_a(c)
-        permute_x(0)
+        def planes(fg):
+            quantize(y_codes[fg][:], y_sc[fg][:], y_grouped[fg][:].rearrange("p l t -> p (l t)"))
+            store_planes(fg, nc.sync)
 
-        last = len(STEPS) - 1
-        tail = STEPS[last]
-        for s, step in enumerate(STEPS[:last]):
-            for ft in range(4):
-                features(step, ft)
-            if 2 <= s <= 5:
-                sketch(s - 2)
-            if s in (7, 8):
-                cross_pair(0, s - 7)
-            if s == 10:
-                cross_pair(1, 0)
-                cross_pair(1, 1)
-            if s >= 1:
-                for h in range(2):
-                    turn(STEPS[s - 1], h, nc.scalar.copy)
-            if s == 1:
-                turn_rows(rows_b, 8, None, cols_b)
-            if 2 <= s <= 5:
-                weigh_sketch(s - 2)
-            if s == 0:
-                prepare_omega()
-                permute_x(1)
-            if s == 1:
-                quantize_omega()
-            if s == 2:
-                permute_x(2)
-            if s == 3:
-                permute_x(3)
-                nc.scalar.copy(out=gain_f[:], in_=gain_bf[:])
-            if s >= 2:
-                quantize_p(STEPS[s - 2])
-            if 3 <= s <= 6:
-                quantize_s(s - 3)
-            if s in (6, 7, 8):
-                scale_prev(s - 6)
-            if s in (7, 8):
-                finish_pair(0, s - 7)
-            if s == 8:
-                store_y(0)
-                interleave(nc.scalar.copy, y_grouped[0][:], y[0][:])
-            if s == 9:
-                planes(0)
-            if s == 10:
-                finish_pair(1, 0)
-                finish_pair(1, 1)
+        nc.vector.memset(rows[:], 0.0)
+        nc.vector.memset(xs_first[:].bitcast(I32), 0)
+        nc.vector.memset(ws_first[:].bitcast(I32), 0)
+        nc.vector.memset(ws_rest[:].bitcast(I32), 0)
+        nc.vector.memset(rows_b[:], 0.0)
+        nc.vector.memset(xs_rest[:].bitcast(I32), 0)
+        make_identity(nc, ident_bf[:])
 
-        fg = NF - 1
-        order = [c for (g, c) in STEPS if g == fg]
+        load_tiles(rows[4:8, 0 : NF * P], offset)
+        load_tiles(rows[0:4, :], a)
+        load_scale_rows(xs_first, xs_view, 0, KP)
+        load_x(nc.scalar, 0)
+        load_w(nc.scalar, 0)
+        load_scale_rows(ws_first, ws_view, 0, KP)
+        load_slices(rows_b[4:8, :], a)
+        load_slices(rows_b[0:4, :], b)
+        load_grouped_rows(om_raw[:], omega)
+        load_w(nc.sync, 1)
+        load_scale_rows(ws_rest, ws_view, KP, F)
+        load_x(nc.sync, 1)
+        load_scale_rows(xs_rest, xs_view, KP, T)
+        load_x(nc.sync, 2)
+        load_x(nc.sync, 3)
+        nc.sync.dma_start(out=gain_bf[:], in_=gain.rearrange("(g p t) -> p g t", p=P, t=4))
+        load_grouped_rows(prev_raw[:], prev)
+        load_w(nc.sync, 2)
+        nc.sync.dma_start(out=off_rest[:], in_=offset[KP:F].partition_broadcast(P))
+
+        turned = turn_rows(rows)
+        nc.scalar.activation(out=cols_bf[:], in_=turned[:, :, 0:8], func=COPY)
+        nc.scalar.copy(out=cols[:], in_=turned[:, :, 4:8])
+        make_identity(nc, ident_f[:])
+
+        last_group = NF - 1
         open_banks = {}
+        half = L // 2
+        y_half = [kept("y_half%d" % h, [P, 4, half], F32) for h in range(2)]
 
         def tail_pass(t, k):
             if k == 0:
                 open_banks[t] = named_bank(("z0", "z1", "acc0", "acc1")[t], [P, L], F32)
-            cross_pass(open_banks[t][:], fg, t, order[k], k)
+            cross_pass(open_banks[t][:], last_group, t, (0, 2, 1, 3)[k], k)
 
+        def quantize_slice(step, t):
+            cols_t = slice(P * t, P * (t + 1))
+            quantize(p_codes[step][:, cols_t], p_sc[step][:, cols_t], grouped[step][:, KP * t : KP * (t + 1)])
+
+        def finish_half(h, t):
+            ls = slice(half * h, half * (h + 1))
+            finish(y_half[h][:, t, :], open_banks[t][:, ls], last_group, t, ls)
+
+        def store_half(h):
+            nc.sync.dma_start(out=out_rows(last_group)[:, :, half * h : half * (h + 1)], in_=y_half[h][:])
+
+        def weave_half(h, engine_copy):
+            interleave(engine_copy, y_grouped[last_group][:, half * h : half * (h + 1), :], y_half[h][:])
+
+        def quantize_half(h):
+            ls = slice(half * h, half * (h + 1))
+            quantize(y_codes[last_group][:, ls], y_sc[last_group][:, ls], y_grouped[last_group][:, ls, :].rearrange("p l t -> p (l t)"))
+
+        nc.scalar.copy(out=off_first[:], in_=spread(0, 4)[:])
+        spread_a(0, nc.scalar.copy)
+        permute_x(0)
+        spread_a(2, nc.scalar.copy)
+        features((0, 0), 0)
+        nc.scalar.copy(out=cols_b[:], in_=turn_rows(rows_b)[:, :, 0:8])
+        make_shift((0, 1), 0)
+        make_shift((0, 1), 1)
+        spread_a(3, nc.scalar.copy)
+        features((0, 0), 1)
+        features((0, 0), 2)
+        prepare_omega()
+        features((0, 0), 3)
+        make_shift((0, 1), 2)
+        features((1, 0), 0)
+        turn((0, 0), 0, 2, nc.scalar.copy)
+        turn((0, 0), 2, 2, nc.scalar.copy)
+        make_shift((0, 1), 3)
+        quantize_omega()
+        permute_x(1)
+        features((1, 0), 1)
+        permute_x(2)
+        features((1, 0), 2)
+        features((1, 0), 3)
+        sketch(0)
+        scale_prev(0, 3)
+        permute_x(3)
+        tokens((0, 1), 0)
+        make_shift((0, 3), 0)
+        weigh_sketch(0)
+        weave_sketch(0)
+        quantize_p((0, 0))
+        turn((1, 0), 0, 2, nc.scalar.copy)
+        turn((1, 0), 2, 2, nc.scalar.copy)
+        tokens((0, 1), 1)
+        make_shift((0, 3), 1)
+        tokens((0, 1), 2)
+        make_shift((0, 3), 2)
+        sketch(1)
+        tokens((0, 1), 3)
+        make_shift((0, 3), 3)
+        weigh_sketch(1)
+        features((0, 2), 0)
+        features((0, 2), 1)
+        features((0, 2), 2)
+        features((0, 2), 3)
+        scale_prev(3, 3)
+        tokens((0, 3), 0)
+        make_shift((1, 1), 0)
+        weave_sketch(1)
+        weave((0, 1), 0, 256, nc.scalar.copy)
+        quantize_p((1, 0))
+        weave((0, 1), 256, 512, nc.scalar.copy)
+        tokens((0, 3), 1)
+        make_shift((1, 1), 1)
+        tokens((0, 3), 2)
+        make_shift((1, 1), 2)
+        sketch(2)
+        weigh_sketch(2)
+        tokens((0, 3), 3)
+        make_shift((1, 1), 3)
+        weave_sketch(2)
+        quantize_s(0)
+        features((1, 2), 0)
+        turn((0, 2), 0, 2, nc.scalar.copy)
+        turn((0, 2), 2, 2, nc.scalar.copy)
+        features((1, 2), 1)
+        quantize_p((0, 2))
+        features((1, 2), 2)
+        features((1, 2), 3)
+        sketch(3)
+        quantize_s(1)
+        weave((0, 3), 0, 256, nc.scalar.copy)
+        weave((0, 3), 256, 512, nc.scalar.copy)
+        quantize_p((0, 1))
+        weigh_sketch(3)
+        quantize_p((0, 3))
+        tokens((1, 1), 0)
+        make_shift((2, 0), 0)
+        weave_sketch(3)
+        quantize_s(2)
+        tokens((1, 1), 1)
+        make_shift((2, 0), 1)
+        turn((1, 2), 0, 2, nc.scalar.copy)
+        turn((1, 2), 2, 2, nc.scalar.copy)
+        tokens((1, 1), 2)
+        make_shift((2, 0), 2)
+        quantize_s(3)
+        tokens((1, 1), 3)
+        make_shift((2, 0), 3)
+        scale_prev(6, 3)
+        weave((1, 1), 0, 256, nc.scalar.copy)
+        features((1, 3), 0)
+        features((1, 3), 1)
+        cross_pair(0, 1)
+        quantize_p((1, 2))
+        features((1, 3), 2)
+        finish_pair(0, 1)
+        weave((1, 1), 256, 512, nc.scalar.copy)
+        features((1, 3), 3)
+        tokens((2, 0), 0)
+        make_shift((2, 1), 0)
+        cross_pair(0, 0)
+        quantize_p((1, 1))
+        turn((1, 3), 0, 2, nc.scalar.copy)
+        finish_pair(0, 0)
+        store_y(0)
+        turn((1, 3), 2, 2, nc.scalar.copy)
+        tokens((2, 0), 1)
+        make_shift((2, 1), 1)
+        tokens((2, 0), 2)
+        make_shift((2, 1), 2)
+        weave_y(0)
+        tokens((2, 0), 3)
+        make_shift((2, 1), 3)
+        features((2, 2), 0)
+        quantize_p((1, 3))
+        features((2, 2), 1)
+        features((2, 2), 2)
+        features((2, 2), 3)
+        weave((2, 0), 0, 256, nc.scalar.copy)
+        weave((2, 0), 256, 512, nc.scalar.copy)
+        cross_pair(1, 0)
+        finish_pair(1, 0)
+        quantize_p((2, 0))
+        tokens((2, 1), 0)
+        scale_prev(9, 3)
+        turn((2, 2), 0, 2, nc.scalar.copy)
+        turn((2, 2), 2, 2, nc.scalar.copy)
+        tokens((2, 1), 1)
+        cross_pair(1, 1)
+        finish_pair(1, 1)
         store_y(1)
-        features(tail, 0)
-        features(tail, 1)
-        for h in range(2):
-            turn(STEPS[last - 1], h, nc.scalar.copy)
-        interleave(nc.scalar.copy, y_grouped[1][:], y[1][:])
-        quantize_p(STEPS[last - 2])
-        features(tail, 2)
-        features(tail, 3)
-        for k in range(2):
-            for t in range(2):
-                tail_pass(t, k)
-        for ft in range(3):
-            turn_one(tail, ft, nc.scalar.copy)
-        quantize_p(STEPS[last - 1])
+        tokens((2, 1), 2)
+        weave_y(1)
+        tokens((2, 1), 3)
+        features((2, 3), 0)
+        weave((2, 1), 0, 256, nc.scalar.copy)
+        weave((2, 1), 256, 512, nc.scalar.copy)
+        planes(0)
+        features((2, 3), 1)
+        quantize_p((2, 2))
+        tail_pass(0, 0)
+        features((2, 3), 2)
+        features((2, 3), 3)
+        turn((2, 3), 0, 2, nc.scalar.copy)
+        quantize_p((2, 1))
+        tail_pass(2, 0)
+        tail_pass(3, 0)
+        turn((2, 3), 2, 1, nc.scalar.copy)
+        turn((2, 3), 3, 1, nc.vector.tensor_copy)
         planes(1)
-        turn_one(tail, 3, nc.scalar.copy)
-        for t, k in ((0, 2), (1, 2), (2, 0), (3, 0), (2, 1), (3, 1), (2, 2), (3, 2)):
-            tail_pass(t, k)
-        for t in range(4):
-            quantize(
-                p_codes[tail][:, P * t : P * (t + 1)], p_sc[tail][:, P * t : P * (t + 1)], grouped[tail][:, KP * t : KP * (t + 1)]
-            )
-        for t in range(4):
-            tail_pass(t, NC - 1)
-        half = L // 2
-        y_half = [kept("y_half%d" % h, [P, 4, half], F32) for h in range(2)]
-        out_rows = out_0[KP * fg : KP * (fg + 1), :].rearrange("(p t) l -> p t l", t=4)
-        for h in range(2):
-            ls = slice(half * h, half * (h + 1))
-            for t in range(4):
-                nc.vector.scalar_tensor_tensor(
-                    out=y_half[h][:, t, :], in0=open_banks[t][:, ls], scalar=gain_f[:, fg, t : t + 1], in1=prev_gain[fg][:, t, ls],
-                    op0=ALU.mult, op1=ALU.add,
-                )
-            nc.sync.dma_start(out=out_rows[:, :, ls], in_=y_half[h][:])
-            interleave(nc.scalar.copy if h == 0 else nc.vector.tensor_copy, y_grouped[fg][:, ls, :], y_half[h][:])
-        for h in range(2):
-            ls = slice(half * h, half * (h + 1))
-            quantize(y_codes[fg][:, ls], y_sc[fg][:, ls], y_grouped[fg][:, ls, :].rearrange("p l t -> p (l t)"))
-        store_planes(fg)
+        quantize_slice((2, 3), 1)
+        quantize_slice((2, 3), 3)
+        tail_pass(0, 1)
+        tail_pass(3, 1)
+        tail_pass(1, 0)
+        tail_pass(1, 1)
+        tail_pass(2, 1)
+        quantize_slice((2, 3), 2)
+        tail_pass(3, 2)
+        tail_pass(2, 2)
+        quantize_slice((2, 3), 0)
+        tail_pass(1, 2)
+        tail_pass(1, 3)
+        finish_half(1, 1)
+        tail_pass(0, 2)
+        finish_half(0, 1)
+        tail_pass(3, 3)
+        finish_half(1, 3)
+        tail_pass(2, 3)
+        finish_half(1, 2)
+        tail_pass(0, 3)
+        finish_half(0, 0)
+        finish_half(1, 0)
+        finish_half(0, 3)
+        finish_half(0, 2)
+        weave_half(1, nc.vector.tensor_copy)
+        quantize_half(1)
+        weave_half(0, nc.scalar.copy)
+        store_half(1)
+        quantize_half(0)
+        store_half(0)
+        store_planes(last_group, nc.scalar)

@@ -57,8 +57,9 @@ def tile_range_finder_transposed_pass_k4_kernel(
         cols_b = kept("cols_b", [P, NC, 8], F32)
         off_first = kept("off_first", [P, KP], BF16)
         off_rest = kept("off_rest", [P, F - KP], BF16)
-        a_wide = {c: kept("a_wide%d" % c, [P, KP], BF16) for c in (0, 2, 3)}
+        a_wide = {c: kept("a_wide%d" % c, [P, KP], BF16) for c in range(NC)}
         gain_bf = kept("gain_bf", [P, NF, 4], BF16)
+        gain_f = kept("gain_f", [P, NF, 4], F32)
         om_raw = kept("om_raw", [P, NG, 4, L], BF16)
         om_grouped = kept("om_grouped", [P, NG, L, 4], BF16)
         om_codes = kept("om_codes", [P, NG, L], U32)
@@ -112,7 +113,7 @@ def tile_range_finder_transposed_pass_k4_kernel(
             nc.sync.dma_start(out=dst.rearrange("p g t l -> p g (t l)"), in_=mat.rearrange("(g p t) l -> p g (t l)", p=P, t=4))
 
         def interleave(engine_copy, dst, src):
-            engine_copy(out=dst.rearrange("p (c i) t -> p c t i", i=4), in_=src.rearrange("p t (c i) -> p c t i", i=4))
+            engine_copy(out=dst, in_=src.rearrange("p t c -> p c t"))
 
         def quantize(codes, scales, grouped):
             nc.vector.quantize_mx(out=codes.bitcast(FP8X4), scales=scales, in_=grouped)
@@ -154,7 +155,7 @@ def tile_range_finder_transposed_pass_k4_kernel(
         def features(step, ft):
             fg, c = step
             if ft == 0:
-                pt[step] = passing("pt", [P, 4, KP], BF16, 3)
+                pt[step] = passing("pt", [P, 4, KP], BF16, 4)
             acc = bank("acc", [P, KP], F32)
             for g in range(NG):
                 nc.tensor.matmul_mx(
@@ -194,19 +195,17 @@ def tile_range_finder_transposed_pass_k4_kernel(
             fg, c = step
             shifts[(step, j)] = passing("shift", [P, KP], F32, 4)
             off = off_first[:] if fg == 0 else off_rest[:, KP * (fg - 1) : KP * fg]
-            nc.gpsimd.tensor_scalar(
+            nc.scalar.activation(
                 out=shifts[(step, j)][:].rearrange("p (t m) -> p t m", t=4),
-                in0=off.rearrange("p (m t) -> p t m", t=4),
-                scalar1=cols_b[:, c, 4 + j : 5 + j],
-                scalar2=0.0,
-                op0=ALU.mult,
-                op1=ALU.add,
+                in_=off.rearrange("p (m t) -> p t m", t=4),
+                func=COPY,
+                scale=cols_b[:, c, 4 + j : 5 + j],
             )
 
         def tokens(step, j):
             fg, c = step
             if j == 0:
-                pt[step] = passing("pt", [P, 4, KP], BF16, 3)
+                pt[step] = passing("pt", [P, 4, KP], BF16, 4)
             acc = bank("acc", [P, KP], F32)
             for g in range(NG):
                 nc.tensor.matmul_mx(
@@ -298,10 +297,7 @@ def tile_range_finder_transposed_pass_k4_kernel(
         def scale_prev(first, count):
             for n in range(first, first + count):
                 fg, t = divmod(n, 4)
-                nc.gpsimd.tensor_scalar(
-                    out=prev_gain[fg][:, t, :], in0=prev_raw[:, fg, t, :], scalar1=gain_bf[:, fg, t : t + 1], scalar2=0.0,
-                    op0=ALU.mult, op1=ALU.add,
-                )
+                nc.scalar.activation(out=prev_gain[fg][:, t, :], in_=prev_raw[:, fg, t, :], func=COPY, scale=gain_f[:, fg, t : t + 1])
 
         def cross_pass(acc, fg, t, c, k):
             nc.tensor.matmul_mx(
@@ -367,7 +363,6 @@ def tile_range_finder_transposed_pass_k4_kernel(
         load_x(nc.scalar, 0)
         load_w(nc.scalar, 0)
         load_scale_rows(ws_first, ws_view, 0, KP)
-        load_slices(rows_b[4:8, :], a)
         load_slices(rows_b[0:4, :], b)
         load_grouped_rows(om_raw[:], omega)
         load_w(nc.sync, 1)
@@ -379,7 +374,6 @@ def tile_range_finder_transposed_pass_k4_kernel(
         nc.sync.dma_start(out=gain_bf[:], in_=gain.rearrange("(g p t) -> p g t", p=P, t=4))
         load_grouped_rows(prev_raw[:], prev)
         load_w(nc.sync, 2)
-        nc.sync.dma_start(out=off_rest[:], in_=offset[KP:F].partition_broadcast(P))
 
         turned = turn_rows(rows)
         nc.scalar.activation(out=cols_bf[:], in_=turned[:, :, 0:8], func=COPY)
@@ -414,187 +408,167 @@ def tile_range_finder_transposed_pass_k4_kernel(
             ls = slice(half * h, half * (h + 1))
             quantize(y_codes[last_group][:, ls], y_sc[last_group][:, ls], y_grouped[last_group][:, ls, :].rearrange("p l t -> p (l t)"))
 
-        nc.scalar.copy(out=off_first[:], in_=spread(0, 4)[:])
         spread_a(0, nc.scalar.copy)
         permute_x(0)
+        spread_a(1, nc.scalar.copy)
         spread_a(2, nc.scalar.copy)
+        prepare_omega()
         features((0, 0), 0)
-        nc.scalar.copy(out=cols_b[:], in_=turn_rows(rows_b)[:, :, 0:8])
-        make_shift((0, 1), 0)
-        make_shift((0, 1), 1)
-        spread_a(3, nc.scalar.copy)
         features((0, 0), 1)
         features((0, 0), 2)
-        prepare_omega()
-        features((0, 0), 3)
-        make_shift((0, 1), 2)
-        features((1, 0), 0)
-        turn((0, 0), 0, 2, nc.scalar.copy)
-        turn((0, 0), 2, 2, nc.scalar.copy)
-        make_shift((0, 1), 3)
+        nc.scalar.copy(out=cols_b[:], in_=turn_rows(rows_b)[:, :, 0:8])
+        spread_a(3, nc.scalar.copy)
         quantize_omega()
-        permute_x(1)
+        features((0, 0), 3)
+        features((1, 0), 0)
         features((1, 0), 1)
-        permute_x(2)
-        features((1, 0), 2)
-        features((1, 0), 3)
         sketch(0)
-        scale_prev(0, 3)
-        permute_x(3)
-        tokens((0, 1), 0)
-        make_shift((0, 3), 0)
         weigh_sketch(0)
         weave_sketch(0)
-        quantize_p((0, 0))
+        permute_x(1)
+        permute_x(2)
+        turn((0, 0), 0, 2, nc.scalar.copy)
+        turn((0, 0), 2, 2, nc.scalar.copy)
         turn((1, 0), 0, 2, nc.scalar.copy)
-        turn((1, 0), 2, 2, nc.scalar.copy)
-        tokens((0, 1), 1)
-        make_shift((0, 3), 1)
-        tokens((0, 1), 2)
-        make_shift((0, 3), 2)
+        features((1, 0), 2)
+        features((1, 0), 3)
+        features((0, 1), 0)
+        features((0, 1), 1)
+        features((0, 1), 2)
+        features((0, 1), 3)
         sketch(1)
-        tokens((0, 1), 3)
-        make_shift((0, 3), 3)
         weigh_sketch(1)
+        weave_sketch(1)
+        permute_x(3)
+        quantize_p((0, 0))
+        quantize_s(0)
+        turn((1, 0), 2, 2, nc.scalar.copy)
+        turn((0, 1), 0, 2, nc.scalar.copy)
+        turn((0, 1), 2, 2, nc.scalar.copy)
         features((0, 2), 0)
         features((0, 2), 1)
         features((0, 2), 2)
         features((0, 2), 3)
-        scale_prev(3, 3)
-        tokens((0, 3), 0)
-        make_shift((1, 1), 0)
-        weave_sketch(1)
-        weave((0, 1), 0, 256, nc.scalar.copy)
-        quantize_p((1, 0))
-        weave((0, 1), 256, 512, nc.scalar.copy)
-        tokens((0, 3), 1)
-        make_shift((1, 1), 1)
-        tokens((0, 3), 2)
-        make_shift((1, 1), 2)
+        features((0, 3), 0)
+        features((0, 3), 1)
         sketch(2)
         weigh_sketch(2)
-        tokens((0, 3), 3)
-        make_shift((1, 1), 3)
         weave_sketch(2)
-        quantize_s(0)
-        features((1, 2), 0)
+        quantize_p((1, 0))
+        quantize_p((0, 1))
+        quantize_s(1)
         turn((0, 2), 0, 2, nc.scalar.copy)
         turn((0, 2), 2, 2, nc.scalar.copy)
-        features((1, 2), 1)
-        quantize_p((0, 2))
-        features((1, 2), 2)
-        features((1, 2), 3)
+        turn((0, 3), 0, 2, nc.scalar.copy)
+        features((0, 3), 2)
+        features((0, 3), 3)
+        features((1, 1), 0)
+        features((1, 1), 1)
+        features((1, 1), 2)
+        features((1, 1), 3)
         sketch(3)
-        quantize_s(1)
-        weave((0, 3), 0, 256, nc.scalar.copy)
-        weave((0, 3), 256, 512, nc.scalar.copy)
-        quantize_p((0, 1))
         weigh_sketch(3)
-        quantize_p((0, 3))
-        tokens((1, 1), 0)
-        make_shift((2, 0), 0)
         weave_sketch(3)
+        quantize_p((0, 2))
         quantize_s(2)
-        tokens((1, 1), 1)
-        make_shift((2, 0), 1)
-        turn((1, 2), 0, 2, nc.scalar.copy)
-        turn((1, 2), 2, 2, nc.scalar.copy)
-        tokens((1, 1), 2)
-        make_shift((2, 0), 2)
+        turn((0, 3), 2, 2, nc.scalar.copy)
+        turn((1, 1), 0, 2, nc.scalar.copy)
+        turn((1, 1), 2, 2, nc.scalar.copy)
+        nc.scalar.copy(out=gain_f[:], in_=gain_bf[:])
+        scale_prev(0, 4)
+        features((1, 2), 0)
+        features((1, 2), 1)
+        features((1, 2), 2)
         quantize_s(3)
-        tokens((1, 1), 3)
-        make_shift((2, 0), 3)
-        scale_prev(6, 3)
-        weave((1, 1), 0, 256, nc.scalar.copy)
+        quantize_p((0, 3))
+        features((1, 2), 3)
         features((1, 3), 0)
         features((1, 3), 1)
-        cross_pair(0, 1)
-        quantize_p((1, 2))
-        features((1, 3), 2)
-        finish_pair(0, 1)
-        weave((1, 1), 256, 512, nc.scalar.copy)
-        features((1, 3), 3)
-        tokens((2, 0), 0)
-        make_shift((2, 1), 0)
         cross_pair(0, 0)
         quantize_p((1, 1))
-        turn((1, 3), 0, 2, nc.scalar.copy)
         finish_pair(0, 0)
+        turn((1, 2), 0, 2, nc.scalar.copy)
+        turn((1, 2), 2, 2, nc.scalar.copy)
+        turn((1, 3), 0, 2, nc.scalar.copy)
+        scale_prev(4, 4)
+        scale_prev(8, 4)
+        features((1, 3), 2)
+        features((1, 3), 3)
+        features((2, 0), 0)
+        features((2, 0), 1)
+        features((2, 0), 2)
+        features((2, 0), 3)
+        cross_pair(0, 1)
+        quantize_p((1, 2))
+        finish_pair(0, 1)
         store_y(0)
         turn((1, 3), 2, 2, nc.scalar.copy)
-        tokens((2, 0), 1)
-        make_shift((2, 1), 1)
-        tokens((2, 0), 2)
-        make_shift((2, 1), 2)
+        turn((2, 0), 0, 2, nc.scalar.copy)
+        turn((2, 0), 2, 2, nc.scalar.copy)
         weave_y(0)
-        tokens((2, 0), 3)
-        make_shift((2, 1), 3)
         features((2, 2), 0)
-        quantize_p((1, 3))
         features((2, 2), 1)
         features((2, 2), 2)
+        quantize_p((1, 3))
         features((2, 2), 3)
-        weave((2, 0), 0, 256, nc.scalar.copy)
-        weave((2, 0), 256, 512, nc.scalar.copy)
+        features((2, 1), 0)
+        features((2, 1), 1)
         cross_pair(1, 0)
-        finish_pair(1, 0)
-        quantize_p((2, 0))
-        tokens((2, 1), 0)
-        scale_prev(9, 3)
-        turn((2, 2), 0, 2, nc.scalar.copy)
-        turn((2, 2), 2, 2, nc.scalar.copy)
-        tokens((2, 1), 1)
         cross_pair(1, 1)
+        quantize_p((2, 0))
+        planes(0)
+        finish_pair(1, 0)
         finish_pair(1, 1)
         store_y(1)
-        tokens((2, 1), 2)
+        turn((2, 2), 0, 2, nc.scalar.copy)
+        turn((2, 2), 2, 2, nc.scalar.copy)
+        turn((2, 1), 0, 2, nc.scalar.copy)
         weave_y(1)
-        tokens((2, 1), 3)
+        features((2, 1), 2)
+        features((2, 1), 3)
         features((2, 3), 0)
-        weave((2, 1), 0, 256, nc.scalar.copy)
-        weave((2, 1), 256, 512, nc.scalar.copy)
-        planes(0)
-        features((2, 3), 1)
         quantize_p((2, 2))
-        tail_pass(0, 0)
+        features((2, 3), 1)
+        planes(1)
         features((2, 3), 2)
         features((2, 3), 3)
+        turn((2, 1), 2, 2, nc.scalar.copy)
         turn((2, 3), 0, 2, nc.scalar.copy)
-        quantize_p((2, 1))
-        tail_pass(2, 0)
-        tail_pass(3, 0)
         turn((2, 3), 2, 1, nc.scalar.copy)
+        quantize_p((2, 1))
         turn((2, 3), 3, 1, nc.vector.tensor_copy)
-        planes(1)
+        quantize_slice((2, 3), 0)
         quantize_slice((2, 3), 1)
+        quantize_slice((2, 3), 2)
         quantize_slice((2, 3), 3)
+        tail_pass(0, 0)
         tail_pass(0, 1)
-        tail_pass(3, 1)
         tail_pass(1, 0)
         tail_pass(1, 1)
-        tail_pass(2, 1)
-        quantize_slice((2, 3), 2)
-        tail_pass(3, 2)
-        tail_pass(2, 2)
-        quantize_slice((2, 3), 0)
-        tail_pass(1, 2)
-        tail_pass(1, 3)
-        finish_half(1, 1)
         tail_pass(0, 2)
-        finish_half(0, 1)
-        tail_pass(3, 3)
-        finish_half(1, 3)
-        tail_pass(2, 3)
-        finish_half(1, 2)
+        tail_pass(1, 2)
         tail_pass(0, 3)
+        tail_pass(1, 3)
+        tail_pass(2, 0)
+        tail_pass(2, 1)
+        tail_pass(2, 2)
+        tail_pass(2, 3)
+        tail_pass(3, 0)
+        tail_pass(3, 1)
+        tail_pass(3, 2)
+        tail_pass(3, 3)
         finish_half(0, 0)
         finish_half(1, 0)
-        finish_half(0, 3)
+        finish_half(0, 1)
+        finish_half(1, 1)
         finish_half(0, 2)
-        weave_half(1, nc.vector.tensor_copy)
-        quantize_half(1)
-        weave_half(0, nc.scalar.copy)
-        store_half(1)
-        quantize_half(0)
+        finish_half(0, 3)
         store_half(0)
+        weave_half(0, nc.scalar.copy)
+        finish_half(1, 2)
+        finish_half(1, 3)
+        store_half(1)
+        weave_half(1, nc.vector.tensor_copy)
+        quantize_half(0)
+        quantize_half(1)
         store_planes(last_group, nc.scalar)

@@ -51,10 +51,11 @@ def tile_range_finder_transposed_pass_k4_kernel(
         ws_rest = kept("ws_rest", [P, NG, F - KP], U8)
         w_sc = [ws_first[:]] + [ws_rest[:, :, KP * g : KP * (g + 1)] for g in range(NF - 1)]
         rows = kept("rows", [P, KP], BF16)
+        b_rows = kept("b_rows", [P, KP], BF16)
         rows_b = kept("rows_b", [P, KP], BF16)
         cols_bf = kept("cols_bf", [P, NC, 8], BF16)
         cols = kept("cols", [P, NC, 4], F32)
-        cols_b = kept("cols_b", [P, NC, 8], F32)
+        cols_b = kept("cols_b", [P, 4, NC], F32)
         off_first = kept("off_first", [P, KP], BF16)
         off_rest = kept("off_rest", [P, F - KP], BF16)
         a_wide = {c: kept("a_wide%d" % c, [P, KP], BF16) for c in range(NC)}
@@ -77,16 +78,12 @@ def tile_range_finder_transposed_pass_k4_kernel(
         ident_bf = kept("ident_bf", [P, P], BF16)
         ident_f = kept("ident_f", [P, P], F32)
 
-        counts = {"acc": 0, "tr": 0, "z": 0}
-        depth = {"acc": 3, "tr": 3, "z": 2}
-
-        def named_bank(tag, shape, dtype):
-            return psum.tile(shape, dtype, name=tag, tag=tag)
+        banks_taken = []
 
         def bank(kind, shape, dtype):
-            tag = "%s%d" % (kind, counts[kind] % depth[kind])
-            counts[kind] += 1
-            return named_bank(tag, shape, dtype)
+            tag = "bank%d" % (len(banks_taken) % 8)
+            banks_taken.append(tag)
+            return psum.tile(shape, dtype, name=tag, tag=tag)
 
         xw_view = x_words.rearrange("g p n t -> p g (n t)")
         ww_view = w_words.rearrange("g p n -> p g n")
@@ -102,9 +99,6 @@ def tile_range_finder_transposed_pass_k4_kernel(
         def load_scale_rows(plane, view, lo, hi):
             for r in range(4):
                 nc.sync.dma_start(out=plane[r:P:32, :, :].bitcast(I32), in_=view[r][:, :, lo:hi].bitcast(I32))
-
-        def load_slices(dst, vec):
-            nc.sync.dma_start(out=dst.rearrange("j (m r) -> j m r", r=8), in_=vec.rearrange("(m j r) -> j m r", j=4, r=8))
 
         def load_tiles(dst, vec):
             nc.sync.dma_start(out=dst.rearrange("f (g p) -> f g p", p=P), in_=vec.rearrange("(g f p) -> f g p", f=4, p=P))
@@ -123,6 +117,11 @@ def tile_range_finder_transposed_pass_k4_kernel(
             for c in range(NC):
                 nc.tensor.transpose(turned[:, c, :], src[:, P * c : P * (c + 1)], ident_bf[:])
             return turned
+
+        def slice_b():
+            nc.scalar.copy(
+                out=rows_b[:].rearrange("p (j q r) -> p j q r", j=4, r=8), in_=b_rows[:].rearrange("p (q j r) -> p j q r", j=4, r=8)
+            )
 
         def spread(block, first):
             wide = bank("tr", [P, 4 * P], BF16)
@@ -284,7 +283,7 @@ def tile_range_finder_transposed_pass_k4_kernel(
                 for u in range(2):
                     j = 2 * e + u
                     nc.scalar.activation(
-                        out=s_rows[c][:, 2 * u + e, :], in_=s_banks[(c, e)][:, u, :], func=COPY, scale=cols_b[:, c, j : j + 1]
+                        out=s_rows[c][:, 2 * u + e, :], in_=s_banks[(c, e)][:, u, :], func=COPY, scale=cols_b[:, j, c : c + 1]
                     )
 
         def weave_sketch(c):
@@ -353,7 +352,7 @@ def tile_range_finder_transposed_pass_k4_kernel(
         nc.vector.memset(xs_first[:].bitcast(I32), 0)
         nc.vector.memset(ws_first[:].bitcast(I32), 0)
         nc.vector.memset(ws_rest[:].bitcast(I32), 0)
-        nc.vector.memset(rows_b[:], 0.0)
+        nc.vector.memset(b_rows[:], 0.0)
         nc.vector.memset(xs_rest[:].bitcast(I32), 0)
         make_identity(nc, ident_bf[:])
 
@@ -363,17 +362,17 @@ def tile_range_finder_transposed_pass_k4_kernel(
         load_x(nc.scalar, 0)
         load_w(nc.scalar, 0)
         load_scale_rows(ws_first, ws_view, 0, KP)
-        load_slices(rows_b[0:4, :], b)
         load_grouped_rows(om_raw[:], omega)
         load_w(nc.sync, 1)
+        nc.sync.dma_start(out=b_rows[0:NC, :], in_=b.rearrange("(c n) -> c n", c=NC))
         load_scale_rows(ws_rest, ws_view, KP, F)
-        load_x(nc.sync, 1)
         load_scale_rows(xs_rest, xs_view, KP, T)
+        load_x(nc.sync, 1)
         load_x(nc.sync, 2)
         load_x(nc.sync, 3)
-        nc.sync.dma_start(out=gain_bf[:], in_=gain.rearrange("(g p t) -> p g t", p=P, t=4))
         load_grouped_rows(prev_raw[:], prev)
         load_w(nc.sync, 2)
+        nc.sync.dma_start(out=gain_bf[:], in_=gain.rearrange("(g p t) -> p g t", p=P, t=4))
 
         turned = turn_rows(rows)
         nc.scalar.activation(out=cols_bf[:], in_=turned[:, :, 0:8], func=COPY)
@@ -387,7 +386,7 @@ def tile_range_finder_transposed_pass_k4_kernel(
 
         def tail_pass(t, k):
             if k == 0:
-                open_banks[t] = named_bank(("z0", "z1", "acc0", "acc1")[t], [P, L], F32)
+                open_banks[t] = bank("z", [P, L], F32)
             cross_pass(open_banks[t][:], last_group, t, (0, 2, 1, 3)[k], k)
 
         def quantize_slice(step, t):
@@ -413,23 +412,23 @@ def tile_range_finder_transposed_pass_k4_kernel(
         spread_a(1, nc.scalar.copy)
         spread_a(2, nc.scalar.copy)
         prepare_omega()
+        slice_b()
         features((0, 0), 0)
         features((0, 0), 1)
         features((0, 0), 2)
-        nc.scalar.copy(out=cols_b[:], in_=turn_rows(rows_b)[:, :, 0:8])
-        spread_a(3, nc.scalar.copy)
-        quantize_omega()
         features((0, 0), 3)
+        quantize_omega()
         features((1, 0), 0)
         features((1, 0), 1)
         sketch(0)
+        nc.scalar.copy(out=cols_b[:], in_=turn_rows(rows_b)[:, :, 0:NC])
         weigh_sketch(0)
-        weave_sketch(0)
         permute_x(1)
-        permute_x(2)
         turn((0, 0), 0, 2, nc.scalar.copy)
         turn((0, 0), 2, 2, nc.scalar.copy)
         turn((1, 0), 0, 2, nc.scalar.copy)
+        spread_a(3, nc.scalar.copy)
+        weave_sketch(0)
         features((1, 0), 2)
         features((1, 0), 3)
         features((0, 1), 0)
@@ -439,13 +438,14 @@ def tile_range_finder_transposed_pass_k4_kernel(
         sketch(1)
         weigh_sketch(1)
         weave_sketch(1)
-        permute_x(3)
+        permute_x(2)
         quantize_p((0, 0))
         quantize_s(0)
         turn((1, 0), 2, 2, nc.scalar.copy)
         turn((0, 1), 0, 2, nc.scalar.copy)
         turn((0, 1), 2, 2, nc.scalar.copy)
         features((0, 2), 0)
+        permute_x(3)
         features((0, 2), 1)
         features((0, 2), 2)
         features((0, 2), 3)

@@ -15,6 +15,7 @@ FP8X4 = mybir.dt.float8_e4m3fn_x4
 FP4X4 = mybir.dt.float4_e2m1fn_x4
 ALU = mybir.AluOpType
 COPY = mybir.ActivationFunctionType.Copy
+IDENTITY = mybir.ActivationFunctionType.Identity
 
 P = 128
 KP = 512
@@ -55,7 +56,7 @@ def tile_range_finder_transposed_pass_k4_kernel(
         rows_b = kept("rows_b", [P, KP], BF16)
         cols_bf = kept("cols_bf", [P, NC, 8], BF16)
         cols = kept("cols", [P, NC, 4], F32)
-        cols_b = kept("cols_b", [P, 4, NC], F32)
+        cols_b = kept("cols_b", [P, 4, 2 * NC], F32)
         off_first = kept("off_first", [P, KP], BF16)
         off_rest = kept("off_rest", [P, F - KP], BF16)
         a_wide = {c: kept("a_wide%d" % c, [P, KP], BF16) for c in range(NC)}
@@ -70,7 +71,7 @@ def tile_range_finder_transposed_pass_k4_kernel(
         p_codes = {s: kept("p_codes%d_%d" % s, [P, KP], U32) for s in blocks}
         p_sc = {s: kept("p_sc%d_%d" % s, [P, KP], U8) for s in blocks}
         prev_raw = kept("prev_raw", [P, NF, 4, L], BF16)
-        prev_gain = [kept("prev_gain%d" % g, [P, 4, L], F32) for g in range(NF)]
+        prev_gain = {NF - 1: kept("prev_gain", [P, 4, L], F32)}
         y = [kept("y%d" % g, [P, 4, L], F32) for g in range(NF - 1)]
         y_grouped = [kept("y_grouped%d" % g, [P, L, 4], BF16) for g in range(NF)]
         y_codes = [kept("y_codes%d" % g, [P, L], U32) for g in range(NF)]
@@ -151,7 +152,7 @@ def tile_range_finder_transposed_pass_k4_kernel(
         grouped = {}
         shifts = {}
 
-        def features(step, ft):
+        def features(step, ft, aside=False):
             fg, c = step
             if ft == 0:
                 pt[step] = passing("pt", [P, 4, KP], BF16, 4)
@@ -166,12 +167,22 @@ def tile_range_finder_transposed_pass_k4_kernel(
                     start=(g == 0),
                     stop=(g == NG - 1),
                 )
+            if aside:
+                shifted = passing("shifted", [P, KP], F32, 2)
+                nc.scalar.activation(
+                    out=shifted[:].rearrange("p (w e) -> p w e", e=2),
+                    in_=acc[:].rearrange("p (e w) -> p w e", e=2),
+                    func=IDENTITY,
+                    bias=cols[:, fg, ft : ft + 1],
+                )
+                nc.gpsimd.tensor_tensor(out=pt[step][:, ft, :], in0=shifted[:], in1=a_wide[c][:], op=ALU.mult)
+                return
             nc.vector.scalar_tensor_tensor(
                 out=pt[step][:, ft, :].rearrange("p (w e) -> p w e", e=2),
                 in0=acc[:].rearrange("p (e w) -> p w e", e=2),
                 scalar=cols[:, fg, ft : ft + 1],
                 in1=a_wide[c][:].rearrange("p (w e) -> p w e", e=2),
-                op0=ALU.subtract,
+                op0=ALU.add,
                 op1=ALU.mult,
             )
 
@@ -193,12 +204,13 @@ def tile_range_finder_transposed_pass_k4_kernel(
         def make_shift(step, j):
             fg, c = step
             shifts[(step, j)] = passing("shift", [P, KP], F32, 4)
-            off = off_first[:] if fg == 0 else off_rest[:, KP * (fg - 1) : KP * fg]
-            nc.scalar.activation(
+            nc.gpsimd.tensor_scalar(
                 out=shifts[(step, j)][:].rearrange("p (t m) -> p t m", t=4),
-                in_=off.rearrange("p (m t) -> p t m", t=4),
-                func=COPY,
-                scale=cols_b[:, c, 4 + j : 5 + j],
+                in0=off_rest[:, KP * (fg - 1) : KP * fg].rearrange("p (m t) -> p t m", t=4),
+                scalar1=cols_b[:, j, NC + c : NC + c + 1],
+                scalar2=0.0,
+                op0=ALU.mult,
+                op1=ALU.add,
             )
 
         def tokens(step, j):
@@ -220,7 +232,7 @@ def tile_range_finder_transposed_pass_k4_kernel(
             nc.vector.scalar_tensor_tensor(
                 out=pt[step][:, 2 * u + e, :].rearrange("p (t m) -> p t m", t=4),
                 in0=acc[:].rearrange("p (m t) -> p t m", t=4),
-                scalar=cols_b[:, c, 4 + j : 5 + j],
+                scalar=cols_b[:, j, NC + c : NC + c + 1],
                 in1=shifts[(step, j)][:].rearrange("p (t m) -> p t m", t=4),
                 op0=ALU.mult,
                 op1=ALU.subtract,
@@ -323,10 +335,18 @@ def tile_range_finder_transposed_pass_k4_kernel(
                 out=dst, in0=acc, scalar=gain_bf[:, fg, t : t + 1], in1=prev_gain[fg][:, t, ls], op0=ALU.mult, op1=ALU.add
             )
 
+        sums = {}
+
         def finish_pair(fg, h):
+            sums[(fg, h)] = passing("z_sum", [P, 2, L], F32, 2)
+            nc.vector.tensor_tensor(
+                out=sums[(fg, h)][:], in0=z_banks[(fg, h)][:], in1=prev_raw[:, fg, 2 * h : 2 * h + 2, :], op=ALU.add
+            )
+
+        def gain_pair(fg, h):
             for i in range(2):
                 t = 2 * h + i
-                finish(y[fg][:, t, :], z_banks[(fg, h)][:, i, :], fg, t, slice(0, L))
+                nc.scalar.activation(out=y[fg][:, t, :], in_=sums[(fg, h)][:, i, :], func=COPY, scale=gain_f[:, fg, t : t + 1])
 
         def out_rows(fg):
             return out_0[KP * fg : KP * (fg + 1), :].rearrange("(p t) l -> p t l", t=4)
@@ -365,6 +385,7 @@ def tile_range_finder_transposed_pass_k4_kernel(
         load_grouped_rows(om_raw[:], omega)
         load_w(nc.sync, 1)
         nc.sync.dma_start(out=b_rows[0:NC, :], in_=b.rearrange("(c n) -> c n", c=NC))
+        nc.sync.dma_start(out=b_rows[NC : 2 * NC, :], in_=a.rearrange("(c n) -> c n", c=NC))
         load_scale_rows(ws_rest, ws_view, KP, F)
         load_scale_rows(xs_rest, xs_view, KP, T)
         load_x(nc.sync, 1)
@@ -373,10 +394,11 @@ def tile_range_finder_transposed_pass_k4_kernel(
         load_grouped_rows(prev_raw[:], prev)
         load_w(nc.sync, 2)
         nc.sync.dma_start(out=gain_bf[:], in_=gain.rearrange("(g p t) -> p g t", p=P, t=4))
+        nc.sync.dma_start(out=off_rest[:], in_=offset[KP:F].partition_broadcast(P))
 
         turned = turn_rows(rows)
         nc.scalar.activation(out=cols_bf[:], in_=turned[:, :, 0:8], func=COPY)
-        nc.scalar.copy(out=cols[:], in_=turned[:, :, 4:8])
+        nc.scalar.activation(out=cols[:], in_=turned[:, :, 4:8], func=COPY, scale=-1.0)
         make_identity(nc, ident_f[:])
 
         last_group = NF - 1
@@ -421,7 +443,7 @@ def tile_range_finder_transposed_pass_k4_kernel(
         features((1, 0), 0)
         features((1, 0), 1)
         sketch(0)
-        nc.scalar.copy(out=cols_b[:], in_=turn_rows(rows_b)[:, :, 0:NC])
+        nc.scalar.copy(out=cols_b[:], in_=turn_rows(rows_b)[:, :, 0 : 2 * NC])
         weigh_sketch(0)
         permute_x(1)
         turn((0, 0), 0, 2, nc.scalar.copy)
@@ -444,117 +466,131 @@ def tile_range_finder_transposed_pass_k4_kernel(
         turn((1, 0), 2, 2, nc.scalar.copy)
         turn((0, 1), 0, 2, nc.scalar.copy)
         turn((0, 1), 2, 2, nc.scalar.copy)
-        features((0, 2), 0)
         permute_x(3)
+        features((0, 2), 0)
         features((0, 2), 1)
         features((0, 2), 2)
+        quantize_s(1)
+        sketch(2)
         features((0, 2), 3)
+        make_shift((1, 1), 0)
+        make_shift((1, 1), 1)
         features((0, 3), 0)
         features((0, 3), 1)
-        sketch(2)
-        weigh_sketch(2)
-        weave_sketch(2)
         quantize_p((1, 0))
-        quantize_p((0, 1))
-        quantize_s(1)
+        weigh_sketch(2)
+        features((0, 3), 2)
         turn((0, 2), 0, 2, nc.scalar.copy)
         turn((0, 2), 2, 2, nc.scalar.copy)
         turn((0, 3), 0, 2, nc.scalar.copy)
-        features((0, 3), 2)
+        weave_sketch(2)
+        make_shift((1, 1), 2)
+        make_shift((1, 1), 3)
+        quantize_p((0, 1))
+        quantize_p((0, 2))
+        nc.scalar.copy(out=gain_f[:], in_=gain_bf[:])
         features((0, 3), 3)
-        features((1, 1), 0)
-        features((1, 1), 1)
-        features((1, 1), 2)
-        features((1, 1), 3)
         sketch(3)
         weigh_sketch(3)
-        weave_sketch(3)
-        quantize_p((0, 2))
-        quantize_s(2)
+        tokens((1, 1), 0)
+        make_shift((1, 3), 0)
+        tokens((1, 1), 1)
+        make_shift((1, 3), 1)
+        tokens((1, 1), 2)
+        make_shift((1, 3), 2)
+        tokens((1, 1), 3)
+        make_shift((1, 3), 3)
         turn((0, 3), 2, 2, nc.scalar.copy)
-        turn((1, 1), 0, 2, nc.scalar.copy)
-        turn((1, 1), 2, 2, nc.scalar.copy)
-        nc.scalar.copy(out=gain_f[:], in_=gain_bf[:])
-        scale_prev(0, 4)
+        weave_sketch(3)
         features((1, 2), 0)
         features((1, 2), 1)
         features((1, 2), 2)
-        quantize_s(3)
-        quantize_p((0, 3))
         features((1, 2), 3)
-        features((1, 3), 0)
-        features((1, 3), 1)
-        cross_pair(0, 0)
-        quantize_p((1, 1))
-        finish_pair(0, 0)
+        quantize_p((0, 3))
+        quantize_s(2)
+        quantize_s(3)
+        weave((1, 1), 0, 256, nc.scalar.copy)
+        weave((1, 1), 256, 512, nc.scalar.copy)
+        tokens((1, 3), 0)
+        make_shift((2, 2), 0)
         turn((1, 2), 0, 2, nc.scalar.copy)
         turn((1, 2), 2, 2, nc.scalar.copy)
-        turn((1, 3), 0, 2, nc.scalar.copy)
-        scale_prev(4, 4)
+        tokens((1, 3), 1)
+        make_shift((2, 2), 1)
+        tokens((1, 3), 2)
+        make_shift((2, 2), 2)
+        cross_pair(0, 0)
+        finish_pair(0, 0)
+        tokens((1, 3), 3)
+        make_shift((2, 2), 3)
         scale_prev(8, 4)
-        features((1, 3), 2)
-        features((1, 3), 3)
+        weave((1, 3), 0, 256, nc.scalar.copy)
+        weave((1, 3), 256, 512, nc.scalar.copy)
         features((2, 0), 0)
+        cross_pair(0, 1)
+        finish_pair(0, 1)
+        gain_pair(0, 0)
+        gain_pair(0, 1)
+        store_y(0)
         features((2, 0), 1)
         features((2, 0), 2)
         features((2, 0), 3)
-        cross_pair(0, 1)
+        quantize_p((1, 1))
         quantize_p((1, 2))
-        finish_pair(0, 1)
-        store_y(0)
-        turn((1, 3), 2, 2, nc.scalar.copy)
+        tokens((2, 2), 0)
+        tokens((2, 2), 1)
+        tokens((2, 2), 2)
+        weave_y(0)
+        quantize_p((1, 3))
+        tokens((2, 2), 3)
         turn((2, 0), 0, 2, nc.scalar.copy)
         turn((2, 0), 2, 2, nc.scalar.copy)
-        weave_y(0)
-        features((2, 2), 0)
-        features((2, 2), 1)
-        features((2, 2), 2)
-        quantize_p((1, 3))
-        features((2, 2), 3)
+        weave((2, 2), 0, 256, nc.scalar.copy)
+        weave((2, 2), 256, 512, nc.scalar.copy)
         features((2, 1), 0)
         features((2, 1), 1)
+        features((2, 1), 2)
+        planes(0)
         cross_pair(1, 0)
         cross_pair(1, 1)
+        turn((2, 1), 0, 2, nc.scalar.copy)
         quantize_p((2, 0))
-        planes(0)
         finish_pair(1, 0)
         finish_pair(1, 1)
+        gain_pair(1, 0)
+        gain_pair(1, 1)
         store_y(1)
-        turn((2, 2), 0, 2, nc.scalar.copy)
-        turn((2, 2), 2, 2, nc.scalar.copy)
-        turn((2, 1), 0, 2, nc.scalar.copy)
-        weave_y(1)
-        features((2, 1), 2)
         features((2, 1), 3)
+        weave_y(1)
         features((2, 3), 0)
-        quantize_p((2, 2))
         features((2, 3), 1)
-        planes(1)
         features((2, 3), 2)
         features((2, 3), 3)
         turn((2, 1), 2, 2, nc.scalar.copy)
         turn((2, 3), 0, 2, nc.scalar.copy)
+        quantize_p((2, 2))
+        turn((2, 3), 3, 1, nc.vector.tensor_copy)
         turn((2, 3), 2, 1, nc.scalar.copy)
         quantize_p((2, 1))
-        turn((2, 3), 3, 1, nc.vector.tensor_copy)
         quantize_slice((2, 3), 0)
         quantize_slice((2, 3), 1)
         quantize_slice((2, 3), 2)
         quantize_slice((2, 3), 3)
+        planes(1)
         tail_pass(0, 0)
-        tail_pass(0, 1)
         tail_pass(1, 0)
+        tail_pass(0, 1)
         tail_pass(1, 1)
-        tail_pass(0, 2)
-        tail_pass(1, 2)
-        tail_pass(0, 3)
-        tail_pass(1, 3)
         tail_pass(2, 0)
+        tail_pass(3, 0)
         tail_pass(2, 1)
+        tail_pass(3, 1)
+        tail_pass(0, 2)
+        tail_pass(0, 3)
+        tail_pass(1, 2)
+        tail_pass(1, 3)
         tail_pass(2, 2)
         tail_pass(2, 3)
-        tail_pass(3, 0)
-        tail_pass(3, 1)
         tail_pass(3, 2)
         tail_pass(3, 3)
         finish_half(0, 0)

from contextlib import ExitStack

import concourse.mybir as mybir
from concourse.masks import make_identity

T, D, F, L = 2048, 1024, 1536, 256
FLOPS = 2 * T * D * F + 2 * T * D * L + 2 * F * T * L

F32 = mybir.dt.float32
BF16 = mybir.dt.bfloat16
I32 = mybir.dt.int32
U32 = mybir.dt.uint32
U8 = mybir.dt.uint8
FP8X4 = mybir.dt.float8_e4m3fn_x4
FP4X4 = mybir.dt.float4_e2m1fn_x4
ALU = mybir.AluOpType
COPY = mybir.ActivationFunctionType.Copy
IDENTITY = mybir.ActivationFunctionType.Identity

P = 128
KP = 512
NG = D // KP
NC = T // KP
NF = F // KP
ALIGN = 256


def tile_range_finder_transposed_pass_k4_kernel(
    tc, x_words, x_scales, w_words, w_scales, omega, offset, a, b, prev, gain, out_0, out_1, out_2
):
    nc = tc.nc
    with ExitStack() as ctx:
        keep = ctx.enter_context(tc.tile_pool(name="keep", bufs=1))
        work = ctx.enter_context(tc.tile_pool(name="work", bufs=3))
        psum = ctx.enter_context(tc.psum_pool(name="psum", bufs=1))
        ctx.enter_context(tc.manual_schedule())

        def kept(name, shape, dtype):
            return keep.tile(shape, dtype, name=name, align_bytes=ALIGN)

        def passing(name, shape, dtype, bufs):
            return work.tile(shape, dtype, name=name, tag=name, align_bytes=ALIGN, bufs=bufs)

        blocks = [(fg, c) for fg in range(NF) for c in range(NC)]
        x_raw = [kept("x_raw%d" % c, [P, NG, KP], U32) for c in range(NC)]
        x_codes = [kept("x_codes%d" % c, [P, NG, KP], U32) for c in range(NC)]
        xs_first = kept("xs_first", [P, NG, KP], U8)
        xs_rest = kept("xs_rest", [P, NG, T - KP], U8)
        x_sc = [kept("x_sc%d" % c, [P, NG, KP], U8) for c in range(NC)]
        w_codes = [kept("w_codes%d" % g, [P, NG, 2 * KP], U8) for g in range(NF)]
        ws_first = kept("ws_first", [P, NG, KP], U8)
        ws_rest = kept("ws_rest", [P, NG, F - KP], U8)
        w_sc = [ws_first[:]] + [ws_rest[:, :, KP * g : KP * (g + 1)] for g in range(NF - 1)]
        rows = kept("rows", [P, KP], BF16)
        b_rows = kept("b_rows", [P, KP], BF16)
        rows_b = kept("rows_b", [P, KP], BF16)
        cols_bf = kept("cols_bf", [P, NC, 8], BF16)
        cols = kept("cols", [P, NC, 4], F32)
        cols_b = kept("cols_b", [P, 4, 2 * NC], F32)
        off_first = kept("off_first", [P, KP], BF16)
        off_rest = kept("off_rest", [P, F - KP], BF16)
        a_wide = {c: kept("a_wide%d" % c, [P, KP], BF16) for c in range(NC)}
        gain_bf = kept("gain_bf", [P, NF, 4], BF16)
        gain_f = kept("gain_f", [P, NF, 4], F32)
        om_raw = kept("om_raw", [P, NG, 4, L], BF16)
        om_grouped = kept("om_grouped", [P, NG, L, 4], BF16)
        om_codes = kept("om_codes", [P, NG, L], U32)
        om_sc = kept("om_sc", [P, NG, L], U8)
        s_codes = [kept("s_codes%d" % c, [P, L], U32) for c in range(NC)]
        s_sc = [kept("s_sc%d" % c, [P, L], U8) for c in range(NC)]
        p_codes = {s: kept("p_codes%d_%d" % s, [P, KP], U32) for s in blocks}
        p_sc = {s: kept("p_sc%d_%d" % s, [P, KP], U8) for s in blocks}
        prev_raw = kept("prev_raw", [P, NF, 4, L], BF16)
        prev_gain = {NF - 1: kept("prev_gain", [P, 4, L], F32)}
        y = [kept("y%d" % g, [P, 4, L], F32) for g in range(NF - 1)]
        y_grouped = [kept("y_grouped%d" % g, [P, L, 4], BF16) for g in range(NF)]
        y_codes = [kept("y_codes%d" % g, [P, L], U32) for g in range(NF)]
        y_sc = [kept("y_sc%d" % g, [P, L], U8) for g in range(NF)]
        ident_bf = kept("ident_bf", [P, P], BF16)
        ident_f = kept("ident_f", [P, P], F32)

        banks_taken = []

        def bank(kind, shape, dtype):
            tag = "bank%d" % (len(banks_taken) % 8)
            banks_taken.append(tag)
            return psum.tile(shape, dtype, name=tag, tag=tag)

        xw_view = x_words.rearrange("g p n t -> p g (n t)")
        ww_view = w_words.rearrange("g p n -> p g n")
        xs_view = x_scales.rearrange("g (Q r) n -> r Q g n", r=4)
        ws_view = w_scales.rearrange("g (Q r) n -> r Q g n", r=4)

        def load_x(queue, c):
            queue.dma_start(out=x_raw[c][:].bitcast(I32), in_=xw_view[:, :, 4 * KP * c : 4 * KP * (c + 1)].bitcast(I32))

        def load_w(queue, g):
            queue.dma_start(out=w_codes[g][:].bitcast(I32), in_=ww_view[:, :, 2 * KP * g : 2 * KP * (g + 1)].bitcast(I32))

        def load_scale_rows(plane, view, lo, hi):
            for r in range(4):
                nc.sync.dma_start(out=plane[r:P:32, :, :].bitcast(I32), in_=view[r][:, :, lo:hi].bitcast(I32))

        def load_tiles(dst, vec):
            nc.sync.dma_start(out=dst.rearrange("f (g p) -> f g p", p=P), in_=vec.rearrange("(g f p) -> f g p", f=4, p=P))

        def load_grouped_rows(dst, mat):
            nc.sync.dma_start(out=dst.rearrange("p g t l -> p g (t l)"), in_=mat.rearrange("(g p t) l -> p g (t l)", p=P, t=4))

        def interleave(engine_copy, dst, src):
            engine_copy(out=dst, in_=src.rearrange("p t c -> p c t"))

        def quantize(codes, scales, grouped):
            nc.vector.quantize_mx(out=codes.bitcast(FP8X4), scales=scales, in_=grouped)

        def turn_rows(src):
            turned = bank("tr", [P, NC, P], BF16)
            for c in range(NC):
                nc.tensor.transpose(turned[:, c, :], src[:, P * c : P * (c + 1)], ident_bf[:])
            return turned

        def slice_b():
            nc.scalar.copy(
                out=rows_b[:].rearrange("p (j q r) -> p j q r", j=4, r=8), in_=b_rows[:].rearrange("p (q j r) -> p j q r", j=4, r=8)
            )

        def spread(block, first):
            wide = bank("tr", [P, 4 * P], BF16)
            for j in range(4):
                column = cols_bf[:, block, first + j : first + j + 1]
                nc.tensor.transpose(wide[:, P * j : P * (j + 1)], column.to_broadcast([P, P]), ident_bf[:])
            return wide

        def spread_a(c, engine_copy):
            engine_copy(
                out=a_wide[c][:].rearrange("p (u q r e) -> p u q r e", e=2, u=2, r=8),
                in_=spread(c, 0)[:].rearrange("p (q e u r) -> p u q r e", e=2, u=2, r=8),
            )

        def permute_x(c):
            nc.vector.tensor_copy(
                out=x_codes[c][:].bitcast(I32).rearrange("p g (j q r) -> p g j q r", j=4, r=8),
                in_=x_raw[c][:].bitcast(I32).rearrange("p g (q j r) -> p g j q r", j=4, r=8),
            )
            raw = xs_first[:] if c == 0 else xs_rest[:, :, KP * (c - 1) : KP * c]
            nc.vector.tensor_copy(
                out=x_sc[c][:].bitcast(I32).rearrange("p g (j q r) -> p g j q r", j=4, r=2),
                in_=raw.bitcast(I32).rearrange("p g (q j r) -> p g j q r", j=4, r=2),
            )

        pt = {}
        grouped = {}
        shifts = {}

        def features(step, ft, aside=False):
            fg, c = step
            if ft == 0:
                pt[step] = passing("pt", [P, 4, KP], BF16, 4)
            acc = bank("acc", [P, KP], F32)
            for g in range(NG):
                nc.tensor.matmul_mx(
                    out=acc[:],
                    lhsT=w_codes[fg][:, g, 2 * P * ft : 2 * P * (ft + 1)].bitcast(FP4X4),
                    lhsT_scale=w_sc[fg][:, g, P * ft : P * (ft + 1)],
                    rhs=x_codes[c][:, g, :].bitcast(FP8X4),
                    rhs_scale=x_sc[c][:, g, :],
                    start=(g == 0),
                    stop=(g == NG - 1),
                )
            if aside:
                shifted = passing("shifted", [P, KP], F32, 2)
                nc.scalar.activation(
                    out=shifted[:].rearrange("p (w e) -> p w e", e=2),
                    in_=acc[:].rearrange("p (e w) -> p w e", e=2),
                    func=IDENTITY,
                    bias=cols[:, fg, ft : ft + 1],
                )
                nc.gpsimd.tensor_tensor(out=pt[step][:, ft, :], in0=shifted[:], in1=a_wide[c][:], op=ALU.mult)
                return
            nc.vector.scalar_tensor_tensor(
                out=pt[step][:, ft, :].rearrange("p (w e) -> p w e", e=2),
                in0=acc[:].rearrange("p (e w) -> p w e", e=2),
                scalar=cols[:, fg, ft : ft + 1],
                in1=a_wide[c][:].rearrange("p (w e) -> p w e", e=2),
                op0=ALU.add,
                op1=ALU.mult,
            )

        def turn(step, first, count, engine_copy):
            if first == 0:
                grouped[step] = passing("grouped", [P, 4 * KP], BF16, 4)
            tr = bank("tr", [P, 2, count * P], F32)
            for i in range(count):
                words = pt[step][:, first + i, :].bitcast(F32)
                for u in range(2):
                    nc.tensor.transpose(tr[:, u, P * i : P * (i + 1)], words[:, P * u : P * (u + 1)], ident_f[:])
            dst = grouped[step][:].bitcast(F32).rearrange("p (t m u) -> p t m u", t=4, u=2)[:, :, 32 * first : 32 * (first + count), :]
            engine_copy(out=dst, in_=tr[:].rearrange("p u (m t) -> p t m u", t=4))

        def turn_all(step):
            for first in (0, 2):
                turn(step, first, 2, nc.scalar.copy)

        def make_shift(step, j):
            fg, c = step
            shifts[(step, j)] = passing("shift", [P, KP], F32, 4)
            nc.gpsimd.tensor_scalar(
                out=shifts[(step, j)][:].rearrange("p (t m) -> p t m", t=4),
                in0=off_rest[:, KP * (fg - 1) : KP * fg].rearrange("p (m t) -> p t m", t=4),
                scalar1=cols_b[:, j, NC + c : NC + c + 1],
                scalar2=0.0,
                op0=ALU.mult,
                op1=ALU.add,
            )

        def tokens(step, j):
            fg, c = step
            if j == 0:
                pt[step] = passing("pt", [P, 4, KP], BF16, 4)
            acc = bank("acc", [P, KP], F32)
            for g in range(NG):
                nc.tensor.matmul_mx(
                    out=acc[:],
                    lhsT=x_codes[c][:, g, P * j : P * (j + 1)].bitcast(FP8X4),
                    lhsT_scale=x_sc[c][:, g, P * j : P * (j + 1)],
                    rhs=w_codes[fg][:, g, :].bitcast(FP4X4),
                    rhs_scale=w_sc[fg][:, g, :],
                    start=(g == 0),
                    stop=(g == NG - 1),
                )
            e, u = divmod(j, 2)
            nc.vector.scalar_tensor_tensor(
                out=pt[step][:, 2 * u + e, :].rearrange("p (t m) -> p t m", t=4),
                in0=acc[:].rearrange("p (m t) -> p t m", t=4),
                scalar=cols_b[:, j, NC + c : NC + c + 1],
                in1=shifts[(step, j)][:].rearrange("p (t m) -> p t m", t=4),
                op0=ALU.mult,
                op1=ALU.subtract,
            )

        def weave(step, lo, hi, engine_copy):
            if lo == 0:
                grouped[step] = passing("grouped", [P, 4 * KP], BF16, 4)
            interleave(engine_copy, grouped[step][:].rearrange("p (f t) -> p f t", t=4)[:, lo:hi, :], pt[step][:, :, lo:hi])

        def by_features(step):
            for ft in range(4):
                features(step, ft)

        def by_tokens(step, following):
            for j in range(4):
                tokens(step, j)
                if following is not None:
                    make_shift(following, j)

        def quantize_p(step):
            quantize(p_codes[step][:], p_sc[step][:], grouped[step][:])

        def prepare_omega():
            for g in range(NG):
                interleave(nc.scalar.copy, om_grouped[:, g, :, :], om_raw[:, g, :, :])

        def quantize_omega():
            quantize(
                om_codes[:].rearrange("p g l -> p (g l)"),
                om_sc[:].rearrange("p g l -> p (g l)"),
                om_grouped[:].rearrange("p g l t -> p (g l t)"),
            )

        s_grouped = {}
        s_banks = {}

        def sketch(c):
            for e in range(2):
                acc = bank("z", [P, 2, L], F32)
                s_banks[(c, e)] = acc
                for u in range(2):
                    j = 2 * e + u
                    for g in range(NG):
                        nc.tensor.matmul_mx(
                            out=acc[:, u, :],
                            lhsT=x_codes[c][:, g, P * j : P * (j + 1)].bitcast(FP8X4),
                            lhsT_scale=x_sc[c][:, g, P * j : P * (j + 1)],
                            rhs=om_codes[:, g, :].bitcast(FP8X4),
                            rhs_scale=om_sc[:, g, :],
                            start=(g == 0),
                            stop=(g == NG - 1),
                        )

        s_rows = {}

        def weigh_sketch(c):
            s_rows[c] = passing("s_rows", [P, 4, L], BF16, 3)
            for e in range(2):
                for u in range(2):
                    j = 2 * e + u
                    nc.scalar.activation(
                        out=s_rows[c][:, 2 * u + e, :], in_=s_banks[(c, e)][:, u, :], func=COPY, scale=cols_b[:, j, c : c + 1]
                    )

        def weave_sketch(c):
            s_grouped[c] = passing("s_grouped", [P, L, 4], BF16, 4)
            interleave(nc.scalar.copy, s_grouped[c][:], s_rows[c][:])

        def quantize_s(c):
            quantize(s_codes[c][:], s_sc[c][:], s_grouped[c][:].rearrange("p l t -> p (l t)"))

        def scale_prev(first, count):
            for n in range(first, first + count):
                fg, t = divmod(n, 4)
                nc.scalar.activation(out=prev_gain[fg][:, t, :], in_=prev_raw[:, fg, t, :], func=COPY, scale=gain_f[:, fg, t : t + 1])

        def cross_pass(acc, fg, t, c, k):
            nc.tensor.matmul_mx(
                out=acc,
                lhsT=p_codes[(fg, c)][:, P * t : P * (t + 1)].bitcast(FP8X4),
                lhsT_scale=p_sc[(fg, c)][:, P * t : P * (t + 1)],
                rhs=s_codes[c][:].bitcast(FP8X4),
                rhs_scale=s_sc[c][:],
                start=(k == 0),
                stop=(k == NC - 1),
            )

        z_banks = {}

        def cross_pair(fg, h):
            acc = bank("z", [P, 2, L], F32)
            for i in range(2):
                for c in range(NC):
                    cross_pass(acc[:, i, :], fg, 2 * h + i, c, c)
            z_banks[(fg, h)] = acc

        def finish(dst, acc, fg, t, ls):
            nc.vector.scalar_tensor_tensor(
                out=dst, in0=acc, scalar=gain_bf[:, fg, t : t + 1], in1=prev_gain[fg][:, t, ls], op0=ALU.mult, op1=ALU.add
            )

        sums = {}

        def finish_pair(fg, h):
            sums[(fg, h)] = passing("z_sum", [P, 2, L], F32, 2)
            nc.vector.tensor_tensor(
                out=sums[(fg, h)][:], in0=z_banks[(fg, h)][:], in1=prev_raw[:, fg, 2 * h : 2 * h + 2, :], op=ALU.add
            )

        def gain_pair(fg, h):
            for i in range(2):
                t = 2 * h + i
                nc.scalar.activation(out=y[fg][:, t, :], in_=sums[(fg, h)][:, i, :], func=COPY, scale=gain_f[:, fg, t : t + 1])

        def out_rows(fg):
            return out_0[KP * fg : KP * (fg + 1), :].rearrange("(p t) l -> p t l", t=4)

        def store_y(fg):
            nc.sync.dma_start(out=out_rows(fg).rearrange("p t l -> p (t l)"), in_=y[fg][:].rearrange("p t l -> p (t l)"))

        def weave_y(fg):
            interleave(nc.scalar.copy, y_grouped[fg][:], y[fg][:])

        def store_planes(fg, second_queue):
            nc.sync.dma_start(out=out_1[fg].rearrange("p l t -> p (l t)").bitcast(I32), in_=y_codes[fg][:].bitcast(I32))
            rows_out = out_2[fg].rearrange("(Q r) l -> r Q l", r=4)
            for r in range(4):
                queue = second_queue if r % 2 else nc.sync
                queue.dma_start(out=rows_out[r].bitcast(I32), in_=y_sc[fg][r:P:32, :].bitcast(I32))

        def planes(fg):
            quantize(y_codes[fg][:], y_sc[fg][:], y_grouped[fg][:].rearrange("p l t -> p (l t)"))
            store_planes(fg, nc.sync)

        nc.vector.memset(rows[:], 0.0)
        nc.vector.memset(xs_first[:].bitcast(I32), 0)
        nc.vector.memset(ws_first[:].bitcast(I32), 0)
        nc.vector.memset(ws_rest[:].bitcast(I32), 0)
        nc.vector.memset(b_rows[:], 0.0)
        nc.vector.memset(xs_rest[:].bitcast(I32), 0)
        make_identity(nc, ident_bf[:])

        load_tiles(rows[4:8, 0 : NF * P], offset)
        load_tiles(rows[0:4, :], a)
        load_scale_rows(xs_first, xs_view, 0, KP)
        load_x(nc.scalar, 0)
        load_w(nc.scalar, 0)
        load_scale_rows(ws_first, ws_view, 0, KP)
        load_grouped_rows(om_raw[:], omega)
        load_w(nc.sync, 1)
        nc.sync.dma_start(out=b_rows[0:NC, :], in_=b.rearrange("(c n) -> c n", c=NC))
        nc.sync.dma_start(out=b_rows[NC : 2 * NC, :], in_=a.rearrange("(c n) -> c n", c=NC))
        load_scale_rows(ws_rest, ws_view, KP, F)
        load_scale_rows(xs_rest, xs_view, KP, T)
        load_x(nc.sync, 1)
        load_x(nc.sync, 2)
        load_x(nc.sync, 3)
        load_grouped_rows(prev_raw[:], prev)
        load_w(nc.sync, 2)
        nc.sync.dma_start(out=gain_bf[:], in_=gain.rearrange("(g p t) -> p g t", p=P, t=4))
        nc.sync.dma_start(out=off_rest[:], in_=offset[KP:F].partition_broadcast(P))

        turned = turn_rows(rows)
        nc.scalar.activation(out=cols_bf[:], in_=turned[:, :, 0:8], func=COPY)
        nc.scalar.activation(out=cols[:], in_=turned[:, :, 4:8], func=COPY, scale=-1.0)
        make_identity(nc, ident_f[:])

        last_group = NF - 1
        open_banks = {}
        half = L // 2
        y_half = [kept("y_half%d" % h, [P, 4, half], F32) for h in range(2)]

        def tail_pass(t, k):
            if k == 0:
                open_banks[t] = bank("z", [P, L], F32)
            cross_pass(open_banks[t][:], last_group, t, (0, 2, 1, 3)[k], k)

        def quantize_slice(step, t):
            cols_t = slice(P * t, P * (t + 1))
            quantize(p_codes[step][:, cols_t], p_sc[step][:, cols_t], grouped[step][:, KP * t : KP * (t + 1)])

        def finish_half(h, t):
            ls = slice(half * h, half * (h + 1))
            finish(y_half[h][:, t, :], open_banks[t][:, ls], last_group, t, ls)

        def store_half(h):
            nc.sync.dma_start(out=out_rows(last_group)[:, :, half * h : half * (h + 1)], in_=y_half[h][:])

        def weave_half(h, engine_copy):
            interleave(engine_copy, y_grouped[last_group][:, half * h : half * (h + 1), :], y_half[h][:])

        def quantize_half(h):
            ls = slice(half * h, half * (h + 1))
            quantize(y_codes[last_group][:, ls], y_sc[last_group][:, ls], y_grouped[last_group][:, ls, :].rearrange("p l t -> p (l t)"))

        spread_a(0, nc.scalar.copy)
        permute_x(0)
        spread_a(1, nc.scalar.copy)
        spread_a(2, nc.scalar.copy)
        prepare_omega()
        slice_b()
        features((0, 0), 0)
        features((0, 0), 1)
        features((0, 0), 2)
        features((0, 0), 3)
        quantize_omega()
        features((1, 0), 0)
        features((1, 0), 1)
        sketch(0)
        nc.scalar.copy(out=cols_b[:], in_=turn_rows(rows_b)[:, :, 0 : 2 * NC])
        weigh_sketch(0)
        permute_x(1)
        turn((0, 0), 0, 2, nc.scalar.copy)
        turn((0, 0), 2, 2, nc.scalar.copy)
        turn((1, 0), 0, 2, nc.scalar.copy)
        spread_a(3, nc.scalar.copy)
        weave_sketch(0)
        features((1, 0), 2)
        features((1, 0), 3)
        features((0, 1), 0)
        features((0, 1), 1)
        features((0, 1), 2)
        features((0, 1), 3)
        sketch(1)
        weigh_sketch(1)
        weave_sketch(1)
        permute_x(2)
        quantize_p((0, 0))
        quantize_s(0)
        turn((1, 0), 2, 2, nc.scalar.copy)
        turn((0, 1), 0, 2, nc.scalar.copy)
        turn((0, 1), 2, 2, nc.scalar.copy)
        permute_x(3)
        features((0, 2), 0)
        features((0, 2), 1)
        features((0, 2), 2)
        quantize_s(1)
        sketch(2)
        features((0, 2), 3)
        make_shift((1, 1), 0)
        make_shift((1, 1), 1)
        features((0, 3), 0)
        features((0, 3), 1)
        quantize_p((1, 0))
        weigh_sketch(2)
        features((0, 3), 2)
        turn((0, 2), 0, 2, nc.scalar.copy)
        turn((0, 2), 2, 2, nc.scalar.copy)
        turn((0, 3), 0, 2, nc.scalar.copy)
        weave_sketch(2)
        make_shift((1, 1), 2)
        make_shift((1, 1), 3)
        quantize_p((0, 1))
        quantize_p((0, 2))
        nc.scalar.copy(out=gain_f[:], in_=gain_bf[:])
        features((0, 3), 3)
        sketch(3)
        weigh_sketch(3)
        tokens((1, 1), 0)
        make_shift((1, 3), 0)
        tokens((1, 1), 1)
        make_shift((1, 3), 1)
        tokens((1, 1), 2)
        make_shift((1, 3), 2)
        tokens((1, 1), 3)
        make_shift((1, 3), 3)
        turn((0, 3), 2, 2, nc.scalar.copy)
        weave_sketch(3)
        features((1, 2), 0)
        features((1, 2), 1)
        features((1, 2), 2)
        features((1, 2), 3)
        quantize_p((0, 3))
        quantize_s(2)
        quantize_s(3)
        weave((1, 1), 0, 256, nc.scalar.copy)
        weave((1, 1), 256, 512, nc.scalar.copy)
        tokens((1, 3), 0)
        make_shift((2, 2), 0)
        turn((1, 2), 0, 2, nc.scalar.copy)
        turn((1, 2), 2, 2, nc.scalar.copy)
        tokens((1, 3), 1)
        make_shift((2, 2), 1)
        tokens((1, 3), 2)
        make_shift((2, 2), 2)
        cross_pair(0, 0)
        finish_pair(0, 0)
        tokens((1, 3), 3)
        make_shift((2, 2), 3)
        scale_prev(8, 4)
        weave((1, 3), 0, 256, nc.scalar.copy)
        weave((1, 3), 256, 512, nc.scalar.copy)
        features((2, 0), 0)
        cross_pair(0, 1)
        finish_pair(0, 1)
        gain_pair(0, 0)
        gain_pair(0, 1)
        store_y(0)
        features((2, 0), 1)
        features((2, 0), 2)
        features((2, 0), 3)
        quantize_p((1, 1))
        quantize_p((1, 2))
        tokens((2, 2), 0)
        tokens((2, 2), 1)
        tokens((2, 2), 2)
        weave_y(0)
        quantize_p((1, 3))
        tokens((2, 2), 3)
        turn((2, 0), 0, 2, nc.scalar.copy)
        turn((2, 0), 2, 2, nc.scalar.copy)
        weave((2, 2), 0, 256, nc.scalar.copy)
        weave((2, 2), 256, 512, nc.scalar.copy)
        features((2, 1), 0)
        features((2, 1), 1)
        features((2, 1), 2)
        planes(0)
        cross_pair(1, 0)
        cross_pair(1, 1)
        turn((2, 1), 0, 2, nc.scalar.copy)
        quantize_p((2, 0))
        finish_pair(1, 0)
        finish_pair(1, 1)
        gain_pair(1, 0)
        gain_pair(1, 1)
        store_y(1)
        features((2, 1), 3)
        weave_y(1)
        features((2, 3), 0)
        features((2, 3), 1)
        features((2, 3), 2)
        features((2, 3), 3)
        turn((2, 1), 2, 2, nc.scalar.copy)
        turn((2, 3), 0, 2, nc.scalar.copy)
        quantize_p((2, 2))
        turn((2, 3), 3, 1, nc.vector.tensor_copy)
        turn((2, 3), 2, 1, nc.scalar.copy)
        quantize_p((2, 1))
        quantize_slice((2, 3), 0)
        quantize_slice((2, 3), 1)
        quantize_slice((2, 3), 2)
        quantize_slice((2, 3), 3)
        planes(1)
        tail_pass(0, 0)
        tail_pass(1, 0)
        tail_pass(0, 1)
        tail_pass(1, 1)
        tail_pass(2, 0)
        tail_pass(3, 0)
        tail_pass(2, 1)
        tail_pass(3, 1)
        tail_pass(0, 2)
        tail_pass(0, 3)
        tail_pass(1, 2)
        tail_pass(1, 3)
        tail_pass(2, 2)
        tail_pass(2, 3)
        tail_pass(3, 2)
        tail_pass(3, 3)
        finish_half(0, 0)
        finish_half(1, 0)
        finish_half(0, 1)
        finish_half(1, 1)
        finish_half(0, 2)
        finish_half(0, 3)
        store_half(0)
        weave_half(0, nc.scalar.copy)
        finish_half(1, 2)
        finish_half(1, 3)
        store_half(1)
        weave_half(1, nc.vector.tensor_copy)
        quantize_half(0)
        quantize_half(1)
        store_planes(last_group, nc.scalar)
